import numpy as np, ml_dtypes
CORES = [5,29,101,125,133,157,229,253]
N = 8
import mx_ref
BF = ml_dtypes.bfloat16
def entries(a):
    return np.ascontiguousarray(a.T).reshape(-1)
def table(e):
    return np.ascontiguousarray(np.reshape(e, (-1, 16)).T).astype(np.int32)
def pick(q, e):
    c = np.concatenate([q[0].reshape(128, -1, 4), np.zeros((128, 1, 4), np.uint8)], axis=1); s = np.concatenate([q[1], np.ones((16, 1), np.uint8)], axis=1)
    return (np.ascontiguousarray(c[:, e].reshape(128, -1)), np.ascontiguousarray(s[:, e]))
def join(*qs):
    return (np.concatenate([q[0] for q in qs], axis=1), np.concatenate([q[1] for q in qs], axis=1))
def put(q, e, v):
    c, s = q[0].reshape(128, -1, 4).copy(), q[1].copy(); c[:, e] = v[0].reshape(128, -1, 4); s[:, e] = v[1]
    return (c.reshape(128, -1), s)
def pk(c, s):
    return (np.ascontiguousarray(c), mx_ref.live(s))
def emit(q):
    return q[0], q[1]
def packed(v, rng):
    q = [mx_ref.quantize(np.ascontiguousarray(v[r])) for r in range(N)]
    return np.stack([a for a, b in q]), np.stack([mx_ref.plane(b, rng) for a, b in q])
def cols(t, e):
    v = np.concatenate([t.reshape(128, -1, 4), np.zeros((128, 1, 4), BF)], axis=1)
    return np.ascontiguousarray(v[:, e]).reshape(128, -1)
def f(rng, *shape):
    return mx_ref.flush((rng.standard_normal(shape, dtype=np.float32) * np.exp2(rng.integers(-2, 3, shape[:-1] + (1,)))).astype(BF))
def wide(rng, *shape, cols=0):
    v = rng.standard_normal(shape, dtype=np.float32) * np.exp2(rng.integers(-12, 13, shape)).astype(np.float32)
    if cols: v *= np.repeat(np.exp2(rng.integers(-cols, cols + 1, shape[:-2] + (1, shape[-1] // 4))) * (rng.random(shape[:-2] + (1, shape[-1] // 4)) > 0.0625), 4, axis=-1).astype(np.float32)
    return mx_ref.flush(v.astype(BF))
T, C, CAPP, M = 128, 512, 16, 64
def first(v):
    z = np.zeros((N, 128, 512), BF); z[:, :, :4] = v; return z
def lists(rng, full=False, one=False, odd=False):
    h = int(rng.integers(0, N)); a = rng.permutation(np.delete(np.arange(N), h))
    sn = np.full((N, N, CAPP), -1)
    for d in range(N):
        m, o = int(rng.integers(1, M + 1)), rng.permutation(N * CAPP)
        if odd: m = 2 * int(rng.integers(0, M // 2)) + 1
        if full:
            w = np.isin(o // CAPP, a[:M // CAPP] if d == h else a[:1]); o = np.concatenate([o[w], o[~w]])
            m = M if d == h else int(rng.integers(CAPP, M + 1))
        if one: o = o[o // CAPP != a[0]]
        if one and d == h: m, o = 1, o[o // CAPP != h]
        o = o[:m]
        sn[o // CAPP, d, o % CAPP] = rng.integers(0, T, m)
    return np.stack([table(sn[s]) for s in range(N)])
def setup_inputs(rng):
    kc, ks = packed(f(rng, N, 128, 4 * C), rng)
    return {"x": f(rng, N, 128, 4 * T), "u": first(f(rng, N, 128, 4)), "w": f(rng, N, 128, 512), "kc": kc, "ks": ks, "sn": lists(rng)}
def setup_inputs_full(rng):
    return {**setup_inputs(rng), "sn": lists(rng, full=True)}
def setup_inputs_high(rng):
    d = setup_inputs(rng); g = np.where(rng.permutation(N) < N // 2, 1, -1).astype(np.float32)[:, None, None]
    p = rng.permutation(N)
    g = g * np.where(p < N // 2, 2.0 ** 24, 2.0 ** -24).astype(np.float32)[:, None, None]
    k = np.where(p == N - 1, 2.0 ** -24, 2.0 ** 24).astype(np.float32)[:, None, None]
    d["u"] = first(((np.abs(f(rng, N, 128, 4).astype(np.float32)) + 1) * k).astype(BF))
    d["kc"], d["ks"] = packed((g * (1 + np.abs(f(rng, N, 128, 4 * C).astype(np.float32)))).astype(BF), rng); return d
def setup_inputs_one(rng):
    return {**setup_inputs(rng), "sn": lists(rng, one=True)}
def setup_inputs_spread(rng):
    d = setup_inputs(rng); d["x"] = wide(rng, N, 128, 4 * T, cols=8)
    d["kc"], d["ks"] = packed(wide(rng, N, 128, 4 * C, cols=8), rng); return d
def setup_inputs_ties(rng):
    d = setup_inputs(rng); v = f(rng, N, 128, C // 8 * 4)
    d["kc"], d["ks"] = packed(np.stack([cols(v[r], rng.permutation(np.arange(C) // 8)) for r in range(N)]), rng)
    d["u"][int(rng.integers(0, N))] = 0
    d["sn"] = lists(rng, odd=True); return d
def scores(u, kc, ks):
    return mx_ref.matmul(mx_ref.quantize(np.ascontiguousarray(u)), pk(kc, ks))[0] + np.float32(0)
def check_inputs(d):
    b = []
    for r in range(N):
        if (d["u"][r][:, 4:].astype(np.float32) != 0).any(): b.append("u")
        e = entries(d["sn"][r])
        m = sum(int((entries(d["sn"][s])[r * CAPP:r * CAPP + CAPP] >= 0).sum()) for s in range(N))
        if e.min() < -1 or e.max() >= T or m < 1 or m > M: b.append("sn")
        try: good = bool(np.isfinite(scores(d["u"][r], d["kc"][r], d["ks"][r])).all())
        except Exception: good = False
        if not good: b.append("kc")
    return b
def reference(x, u, w, kc, ks, sn):
    oc, osc, ev = np.zeros((N, 128, 4 * C), np.uint8), np.zeros((N, 16, C), np.uint8), np.zeros((N, 2, M), np.float32)
    y = np.zeros((N, 128, C), np.float32)
    new = join(*[mx_ref.quantize(np.ascontiguousarray(x[s])) for s in range(N)])
    for d in range(N):
        e = []
        for s in range(N):
            v = entries(sn[s])[d * CAPP:d * CAPP + CAPP]; e.append(s * T + v[v >= 0])
        e = np.concatenate(e); m = e.size
        z = scores(u[d], kc[d], ks[d])
        out = np.argsort(z, kind="stable")[:m]
        after = put(pk(kc[d], ks[d]), out, pick(new, e))
        oc[d], osc[d] = emit(after)
        ev[d, 0] = -1; ev[d, 0, :m] = out; ev[d, 1, :m] = z[out]
        y[d] = mx_ref.matmul(mx_ref.quantize(np.ascontiguousarray(w[d])), after)
    return {"oc": oc, "osc": osc, "ev": ev, "y": y}

@@ -1,0 +1,366 @@
+from concourse.bass import DstId, RemoteDMATransfer
+from concourse.mybir import dt, AluOpType as A, AxisListType as AX, ActivationFunctionType as F
+
+CODES, PLANE = "float8_e4m3fn_x4", "uint8"
+
+
+def _f32(n):
+    return ("sbuf", [128, n], "float32")
+
+
+_I1 = ("sbuf", [128, 1], "int32")
+SCRATCH = {
+    "snd": ("dram", [128, 1], "int32"), "snr": ("sbuf", [128, 8], "int32"), "xt": ("sbuf", [128, 520], "bfloat16"),
+    "ut": ("sbuf", [128, 512], "bfloat16"), "wt": ("sbuf", [128, 512], "bfloat16"),
+    "xq": ("sbuf", [128, 130], CODES), "xs": ("sbuf", [128, 130], PLANE),
+    "uq": ("sbuf", [128, 128], CODES), "us": ("sbuf", [128, 128], PLANE),
+    "ur": ("sbuf", [128, 128], CODES), "urs": ("sbuf", [128, 128], PLANE),
+    "wq": ("sbuf", [128, 128], CODES), "ws": ("sbuf", [128, 128], PLANE),
+    "kq": ("sbuf", [128, 576], CODES), "kp": ("sbuf", [128, 576], PLANE),
+    "pq": ("sbuf", [128, 128], CODES), "ps": ("sbuf", [128, 128], PLANE),
+    "fwl": ("dram", [128, 1], "int32"), "fwq": ("sbuf", [128, 32], CODES), "fws": ("sbuf", [128, 32], PLANE),
+    "land": ("dram", [8, 128, 1], "int32"), "row": ("sbuf", [128, 1024], "int32"),
+    "lq": ("sbuf", [128, 128], CODES), "ls": ("sbuf", [128, 128], PLANE),
+    "oq": ("sbuf", [128, 512], CODES), "op": ("sbuf", [128, 512], PLANE),
+    "lst": ("sbuf", [128, 8], "uint16"), "lo": ("sbuf", [128, 2], "uint16"),
+    "zo": ("sbuf", [128, 8], "uint16"), "coff": ("sbuf", [128, 4], "uint16"),
+    "loff": ("sbuf", [128, 32], "uint16"), "roff": ("sbuf", [128, 16], "uint16"),
+    "qall": ("sbuf", [128, 2], "uint16"), "qown": ("sbuf", [128, 2], "uint16"),
+    "pi": _I1, "pm": _I1, "pm32": _I1, "ia": _I1, "ib": _I1, "ic": _I1, "id5": _I1,
+    "pmf": _f32(1), "fa": _f32(1), "fx": _f32(1), "fc": _f32(1), "fd": _f32(1), "is0": _f32(1), "nm": _f32(1),
+    "q16": _f32(32), "jw": _f32(32), "kb": _f32(4), "zr": _f32(128), "k64": _f32(64), "jio": _f32(128), "jrow": _f32(128),
+    "c0": ("sbuf", [128, 640], "bfloat16"), "c1": ("sbuf", [128, 640], "bfloat16"),
+    "c2": ("sbuf", [128, 640], "bfloat16"), "c3": ("sbuf", [128, 640], "bfloat16"),
+    "junk": ("sbuf", [128, 640], "bfloat16"), "junv": ("sbuf", [128, 128], "bfloat16"),
+    "tb": _f32(448), "tt": _f32(128), "rin": _f32(32), "rwp": _f32(32), "l1": _f32(32), "l2": _f32(32), "l3": _f32(32),
+    "fl": _f32(128), "pin1": _f32(128), "pinc": _f32(128), "zq": _f32(4), "zv": _f32(4), "m64": _f32(64),
+    "evi": _f32(128), "ev2": _f32(128), "evw": _f32(512), "ep": _f32(256), "e1": _f32(128), "e2": _f32(64), "e3": _f32(64),
+    "e4": _f32(64), "yb": _f32(512),
+    "pr": ("psum", [128, 512], "float32"), "pc": ("psum", [128, 2048], "float32"),
+    "p2": ("psum", [128, 512], "float32"), "py": ("psum", [128, 1024], "float32"),
+}
+SEMAPHORES = ["sv", "ss", "st", "sg", "dsn", "dsd", "dx", "du", "dk", "dw", "down", "drow", "dr", "dev", "dout",
+              "aL", "aC", "aS", "fC", "fS", "loc"]
+
+
+def bits(es):
+    m = 0
+    for e in es:
+        m |= 1 << e
+    return m
+
+
+def u8(v):
+    return v.bitcast(dt.uint8)
+
+
+def u32(v):
+    return v.bitcast(dt.uint32)
+
+
+def split(es, n, turn=0):
+    if n == 1:
+        return [es]
+    h = len(es) // 2
+    if n == 2:
+        return [es[:h], es[h:]]
+    q = h // 2
+    wide, rest = (es[:h], [es[h:h + q], es[h + q:]]) if turn % 2 == 0 else (es[h:], [es[:q], es[q:h]])
+    return rest[:turn] + [wide] + rest[turn:]
+
+
+def plan(s, T, topo):
+    core = T.cores[s]
+    n = len(T.cores)
+    cross = [d for d in range(n) if d != s and not topo.may_write(core, T.cores[d])]
+    home = [d for d in range(n) if d not in cross]
+    same = [d for d in home if d != s]
+    chip = [f for f in topo.cores_of(core) if f != core]
+    ports = [f for f in chip if all(topo.may_write(f, T.cores[d]) for d in cross)]
+    near = [f for f in ports if topo.die(f) == topo.die(core)]
+    far = [f for f in ports if topo.die(f) != topo.die(core)]
+    a, b = (near, far) if (s // 2) % 2 == 0 else (far, near)
+    off = topo.engines(core, T.cores[same[0]])
+    on = [e for e in topo.engines(core, near[0]) if e not in off]
+    h = len(on) // 2
+    hop = [(k, es, f, ds) for i, k in enumerate("CS") for es, f, ds in ((on[:h], a[i], cross[:2]), (on[h:], b[i], cross[2:]))]
+    straight = [(k, es, d) for i, k in enumerate("CS") for es, d in zip(split(off, 3, i), same)]
+    return {"core": core, "cross": cross, "home": home, "same": same, "order": cross + home, "on": on, "off": off,
+            "list": list(zip([a[0], a[1], b[0], b[1]], cross)), "hop": hop, "straight": straight}
+
+
+def last_leg(f, ds, T, topo):
+    return split(topo.engines(f, T.cores[ds[0]]), len(ds))
+
+
+def xfer(src_core, dst_cores, es, sem, src, dsts, topo):
+    ids = []
+    for d in dst_cores:
+        rid, pid = topo.addr(d, src_core)
+        ids.append(DstId(rid=rid, pnc=pid))
+    return RemoteDMATransfer(dst_ids=ids, dma_engine_mask=bits(es), remote_sem=sem, srcs=[src], dsts=dsts)
+
+
+def part(T, k, codes, plane, i, n):
+    return u8(T[codes][:, 16 * i:16 * (i + n)]) if k == "C" else T[plane][:, 16 * i:16 * (i + n)]
+
+
+def forward(g, core, s, T, topo):
+    p = plan(s, T, topo)
+    loc = 0
+    for f, d in p["list"]:
+        if f == core:
+            es = topo.engines(core, T.cores[d])[:1]
+            g.wait_ge(T.sem.aL, 1)
+            g.remote_dma_fused([xfer(core, [T.cores[d]], es, T.sem.aL, T.fwl[:, :], [T.land[s]], topo)], local_sem=T.sem.loc)
+            loc += len(es)
+    for k, es, f, ds in p["hop"]:
+        if f == core:
+            g.wait_ge(T.sem["f" + k], len(es))
+            ts = []
+            for i, (d, me) in enumerate(zip(ds, last_leg(core, ds, T, topo))):
+                ts.append(xfer(core, [T.cores[d]], me, T.sem["a" + k], part(T, k, "fwq", "fws", i, 1),
+                               [part(T, k, "lq", "ls", s, 1)], topo))
+                loc += len(me)
+            g.remote_dma_fused(ts, local_sem=T.sem.loc)
+    if loc:
+        g.wait_ge(T.sem.loc, loc)
+
+
+def rank_program(g, core, T, topo):
+    r = T.rank_of(core)
+    n = len(T.cores)
+    if r is None:
+        for s in range(n):
+            if T.cores[s] in topo.cores_of(core):
+                forward(g, core, s, T, topo)
+        return
+    P = plan(r, T, topo)
+    V, S, E, Y = g.vector, g.scalar, g.tensor, g.sync
+    sem = T.sem
+    queue = {"v": V, "s": S, "t": E, "g": g, "y": Y}
+    cnt = {"v": 0, "s": 0, "t": 0, "g": 0}
+    seen = {}
+
+    def w(name, *tags):
+        for sn, val in tags:
+            if seen.get((name, sn), 0) < val:
+                queue[name].wait_ge(sem[sn], val)
+                seen[(name, sn)] = val
+
+    def do(name, call, tags):
+        w(name, *tags)
+        call().then_inc(sem["s" + name], 1)
+        cnt[name] += 1
+        return ("s" + name, cnt[name])
+
+    def v(call, *tags):
+        return do("v", call, tags)
+
+    def sc(call, *tags):
+        return do("s", call, tags)
+
+    def mm(call, *tags):
+        return do("t", call, tags)
+
+    def gg(call, *tags):
+        return do("g", call, tags)
+
+    need = {"L": n - 1, "C": 0, "S": 0}
+    for s in range(n):
+        if s == r:
+            continue
+        p = plan(s, T, topo)
+        for k, es, f, ds in p["hop"]:
+            if r in ds:
+                need[k] += len(last_leg(f, ds, T, topo)[ds.index(r)])
+        for k, es, d in p["straight"]:
+            if d == r:
+                need[k] += len(es)
+
+    Y.dma_start(T.snd[:, :], T.sn[:, :]).then_inc(sem.dsd, 16)
+    S.dma_start(T.xt[:, 8:520], T.x[:, :]).then_inc(sem.dx, 16)
+    for k in range(8):
+        (Y if k < 4 else S).dma_start(T.snr[16 * k:16 * k + 16, :], T.sn[:, :]).then_inc(sem.dsn, 16)
+    Y.dma_start(T.ut[:, 0:8], T.u[:, 0:8]).then_inc(sem.du, 16)
+    S.dma_start(T.kp[:, 64:576], T.ks[:, :]).then_inc(sem.dk, 16)
+    Y.dma_start(u8(T.kq[:, 64:576]), T.kc[:, :]).then_inc(sem.dk, 16)
+    Y.dma_start(T.wt[:, :], T.w[:, :]).then_inc(sem.dw, 16)
+    Y.dma_start(T.land[r], T.sn[:, :]).then_inc(sem.down, 16)
+    SN, DX, DU, DK, DW = ("dsn", 128), ("dx", 16), ("du", 16), ("dk", 32), ("dw", 16)
+
+    a_x0 = v(lambda: V.memset(T.xt[:, 0:8], 0.0))
+    a_u0 = v(lambda: V.memset(T.ut[:, 8:512], 0.0))
+    a_zo = v(lambda: V.memset(T.zo[:, :], 0))
+    a_pi = gg(lambda: g.iota(T.pi[:, :], [[1, 1]], 0, 1))
+    a_q16 = gg(lambda: g.iota(T.q16[:, :], [[16, 32]], 0, 0, allow_small_or_imprecise_dtypes=True))
+    a_jio = gg(lambda: g.iota(T.jio[:, :], [[1, 128]], 1, 4, allow_small_or_imprecise_dtypes=True))
+    t1 = v(lambda: V.tensor_scalar(T.ia[:, :], T.pi[:, :], 1, 3, A.logical_shift_right, A.bitwise_and), a_pi)
+    t2 = v(lambda: V.tensor_scalar(T.ib[:, :], T.pi[:, :], 1, None, A.bitwise_and))
+    t3 = v(lambda: V.tensor_scalar(T.ic[:, :], T.pi[:, :], 3, 1, A.logical_shift_right, A.bitwise_and))
+    t4 = v(lambda: V.tensor_scalar(T.id5[:, :], T.pi[:, :], 5, None, A.logical_shift_right))
+    t1 = v(lambda: V.tensor_scalar(T.fa[:, :], T.ia[:, :], 8, None, A.mult), t1)
+    t3 = v(lambda: V.tensor_scalar(T.fc[:, :], T.ic[:, :], 2, None, A.mult), t3)
+    t5 = v(lambda: V.tensor_scalar(T.pm32[:, :], T.pi[:, :], 31, None, A.bitwise_and))
+
+    cx, hm = P["cross"], P["home"]
+    stx, sth = cx[1] - cx[0], hm[1] - hm[0]
+    a_lx = v(lambda: V.tensor_scalar(T.lst[:, 0:4], T.snr[:, cx[0]:cx[0] + 3 * stx + 1:stx], 2, None, A.add), SN)
+    a_ly = v(lambda: V.tensor_scalar(T.lst[:, 4:8], T.snr[:, hm[0]:hm[0] + 3 * sth + 1:sth], 2, None, A.add))
+    a_lo = v(lambda: V.tensor_scalar(T.lo[:, 0:1], T.snr[:, r:r + 1], 2, None, A.add))
+    a_xq = v(lambda: V.quantize_mx(T.xq[:, 0:130], T.xs[:, 0:130], T.xt[:, 0:520]), DX, a_x0)
+
+    def pick(o, oc, i, ic, off, lc, vt, st):
+        x = v(lambda: V.tensor_copy(u32(T[o[0]][:, oc[0]:oc[1]]), u32(T[i[0]][:, ic[0]:ic[1]]).indirect(T[off][:, lc[0]:lc[1]])), *vt)
+        y = sc(lambda: S.activation(T[o[1]][:, oc[0]:oc[1]], T[i[1]][:, ic[0]:ic[1]].indirect(T[off][:, lc[0]:lc[1]]), F.Copy), *st)
+        return x, y
+
+    X, XW = ("xq", "xs"), (0, 130)
+    px = pick(("pq", "ps"), (0, 64), X, XW, "lst", (0, 4), (a_xq, a_lx), (a_xq, a_lx))
+    py = pick(("pq", "ps"), (64, 128), X, XW, "lst", (4, 8), (a_ly,), (a_ly,))
+
+    loc = 0
+
+    def send(ts, es):
+        g.remote_dma_fused(ts, local_sem=sem.loc)
+        return sum(len(e) for e in es)
+
+    def hop(k):
+        calls = [c for c in P["hop"] if c[0] == k]
+        return send([xfer(core, [f], es, sem["f" + k], part(T, k, "pq", "ps", P["order"].index(ds[0]), 2),
+                          [part(T, k, "fwq", "fws", 0, 2)], topo) for _, es, f, ds in calls], [c[1] for c in calls])
+
+    def straight(k):
+        calls = [c for c in P["straight"] if c[0] == k]
+        return send([xfer(core, [T.cores[d]], es, sem["a" + k], part(T, k, "pq", "ps", P["order"].index(d), 1),
+                          [part(T, k, "lq", "ls", r, 1)], topo) for _, es, d in calls], [c[1] for c in calls])
+
+    w("g", ("dsd", 16))
+    fs = [f for f, d in P["list"]]
+    le = [P["on"][:1], P["off"][:1]]
+    loc += send([xfer(core, fs, le[0], sem.aL, T.snd[:, :], [T.fwl[:, :] for f in fs], topo),
+                 xfer(core, [T.cores[d] for d in P["same"]], le[1], sem.aL, T.snd[:, :], [T.land[r] for d in P["same"]], topo)], le)
+    w("g", px[0])
+    loc += hop("C")
+    w("g", px[1])
+    loc += hop("S")
+    w("g", py[0])
+    loc += straight("C")
+    w("g", py[1])
+    loc += straight("S")
+
+    a_uq = v(lambda: V.quantize_mx(T.uq[:, :], T.us[:, :], T.ut[:, :]), DU, a_u0)
+    ur = pick(("ur", "urs"), (0, 128), ("uq", "us"), (0, 128), "zo", (0, 8), (a_uq, a_zo), (a_uq, a_zo))
+    po = pick(("lq", "ls"), (16 * r, 16 * r + 16), X, XW, "lo", (0, 1), (a_lo,), (a_lo,))
+    a_row = mm(lambda: E.matmul_mx(T.pr[:, :], T.ur[:, :], T.urs[:, :], T.kq[:, 64:576], T.kp[:, 64:576], True, True), DK, *ur)
+    turn = (1, 2, 3, 0)
+    a_col = {}
+    for c in turn:
+        lo, hi = 64 + 128 * c, 192 + 128 * c
+        a_col[c] = mm(lambda: E.matmul_mx(T.pc[:, 512 * c:512 * c + 128], T.kq[:, lo:hi], T.kp[:, lo:hi],
+                                          T.ur[:, :], T.urs[:, :], True, True))
+    a_row2 = mm(lambda: E.matmul_mx(T.p2[:, :], T.ur[:, :], T.urs[:, :], T.kq[:, 64:576], T.kp[:, 64:576], True, True))
+    a_tin = v(lambda: V.memset(T.tb[:, 320:448], 0.0))
+    t1 = v(lambda: V.tensor_tensor(T.fx[:, :], T.fa[:, :], T.ib[:, :], A.add), t1, t2)
+    t = v(lambda: V.tensor_scalar(T.pm[:, :], T.pi[:, :], 15, None, A.bitwise_and))
+    t4 = v(lambda: V.tensor_scalar(T.fd[:, :], T.id5[:, :], 2, None, A.mult), t4)
+    a_pm = v(lambda: V.tensor_scalar(T.qall[:, 0:1], T.fx[:, :], T.fc[:, 0:1], None, A.add), t1, t3)
+    a_pm = v(lambda: V.tensor_scalar(T.qall[:, 1:2], T.fx[:, :], T.fc[:, 0:1], 4.0, A.add, A.add))
+    t = v(lambda: V.tensor_copy(T.pmf[:, :], T.pm[:, :]), t)
+    a_pq = v(lambda: V.tensor_scalar(T.qown[:, 0:1], T.fx[:, :], T.fd[:, 0:1], None, A.add), t4)
+    a_nm = v(lambda: V.tensor_scalar(T.nm[:, :], T.pm32[:, :], 0, None, A.is_gt), t5)
+    a_is0 = v(lambda: V.tensor_scalar(T.is0[:, :], T.pm32[:, :], 0, None, A.is_equal))
+
+    sums = []
+    for c in turn:
+        b = T["c%d" % c]
+        sj = T.pc[:, 512 * c:512 * c + 1]
+        own = T.pr[:, 128 * c:128 * c + 128]
+        t0 = v(lambda: V.tensor_scalar(b[:, 512:640], own, sj, None, A.is_equal), a_row, a_col[c])
+        masked = gg(lambda: g.affine_select(b[:, 512:640], b[:, 512:640], [[-1, 128]], A.is_gt, 0.0, 0, 1), t0)
+        if c:
+            v(lambda: V.tensor_scalar(b[:, 0:128 * c], T.pr[:, 0:128 * c], sj, None, A.is_le))
+        t0 = v(lambda: V.tensor_scalar(b[:, 128 * c:512], T.pr[:, 128 * c:512], sj, None, A.is_lt))
+        if c:
+            sums.append(sc(lambda: S.activation(T.junk[:, :], b[:, :], F.Copy, accum_out=T.tb[:, 320 + 32 * c:321 + 32 * c]),
+                           t0, masked, a_tin, *sums[-1:]))
+        else:
+            sums.append(v(lambda: V.tensor_tensor_scan(T.tb[:, 1:321], b[:, 0:320], b[:, 320:640], 0.0, A.add, A.add),
+                          t0, masked, a_tin))
+    a_k64 = gg(lambda: g.iota(T.k64[:, :], [[1, 64]], 0, 0, allow_small_or_imprecise_dtypes=True))
+    w("y", ("aL", need["L"]), ("down", 16))
+    Y.dma_start(T.row[0:1, :], T.land[:, :, :]).then_inc(sem.drow, 16)
+    a_tt = v(lambda: V.transpose(T.tt[:, :], T.tb[:, 320:448]), *sums)
+    for a in range(4):
+        nm = "sy"[a % 2]
+        w(nm, a_tt)
+        queue[nm].dma_start(T.rin[32 * a:32 * a + 32, 0:16], T.tt[0:128:32, :]).then_inc(sem.dr, 16)
+    a_kb = v(lambda: V.tensor_scalar(T.kb[:, :], T.q16[:, 0:4], T.pmf[:, 0:1], 0.5, A.add, A.add), t, a_q16)
+    a_jw = v(lambda: V.tensor_scalar(T.jw[:, :], T.q16[:, :], T.pmf[:, 0:1], 64.0, A.add, A.add))
+    a_zr = v(lambda: V.memset(T.zr[0:1, :], 0.0))
+    for a in range(4):
+        a_evi = sc(lambda: S.activation(T.evi[32 * a:32 * a + 32, :], T.p2[32 * a:32 * a + 32, 128 * a:128 * a + 128], F.Identity,
+                                        scale=T.nm[32 * a:32 * a + 32, 0:1]), a_row2, a_nm)
+    a_wq = v(lambda: V.quantize_mx(T.wq[:, :], T.ws[:, :], T.wt[:, :]), DW)
+
+    t = v(lambda: V.tensor_scalar(T.fl[0:1, :], T.row[0:1, r:1024:8], 0, None, A.is_ge), ("drow", 16))
+    t = v(lambda: V.tensor_tensor_scan(T.pin1[0:1, :], T.fl[0:1, :], T.zr[0:1, :], 0.0, A.add, A.add), t, a_zr)
+    a_pinc = gg(lambda: g.partition_broadcast(T.pinc[:, :], T.pin1[0:1, :], 128), t)
+    m = T.pinc[:, 127:128]
+    a_z = sums[2]
+    for q in range(3):
+        a_z = sc(lambda: S.activation(T.junk[:, 0:127], T.pinc[:, 0:127], F.Sign, bias=T.kb[:, q:q + 1], scale=-1.0,
+                                      accum_out=T.zq[:, q:q + 1]), a_pinc, a_kb, a_z)
+    a_jr = v(lambda: V.tensor_scalar(T.jrow[:, :], T.jio[:, :], T.is0[:, 0:1], None, A.mult), a_jio, a_is0)
+    a_w0 = v(lambda: V.memset(T.evw[:, 0:64], 0.0))
+    a_ev2 = v(lambda: V.tensor_tensor(T.ev2[:, :], T.evi[:, :], T.jrow[:, :], A.add), a_evi, a_jr)
+    t1 = v(lambda: V.tensor_scalar(T.junv[:, 0:127], T.pinc[:, 0:127], T.kb[:, 3:4], None, A.is_le), a_pinc)
+    a_m64 = v(lambda: V.tensor_scalar(T.m64[0:2, :], T.k64[0:2, :], T.pinc[0:2, 127:128], None, A.is_lt), a_k64)
+    t1 = v(lambda: V.tensor_reduce(T.zv[:, 0:1], T.junv[:, 0:127], AX.X, A.add), t1)
+    t = v(lambda: V.tensor_copy(T.rin[:, 16:32], T.rin[:, 0:16]), ("dr", 64))
+    a_c3 = v(lambda: V.tensor_copy(T.coff[:, 3:4], T.zv[:, 0:1]), t1)
+    a_rwp = v(lambda: V.transpose(T.rwp[:, :], T.rin[:, :]), t)
+    t = v(lambda: V.tensor_scalar(T.l1[:, :], T.rwp[:, :].indirect(T.qall[:, 0:2]), m, 2048.0, A.is_ge, A.mult), a_rwp, a_pm)
+    a_roff = v(lambda: V.tensor_copy(T.roff[:, :], T.rwp[:, :].indirect(T.qown[:, 0:1])), a_pq)
+    t = v(lambda: V.tensor_tensor(T.l2[:, :], T.rwp[:, :].indirect(T.qall[:, 0:2]), T.l1[:, :], A.max), t)
+    t = v(lambda: V.tensor_tensor(T.l3[:, :], T.l2[:, :], T.jw[:, :], A.min), t, a_jw)
+    a_ev = v(lambda: V.tensor_copy(T.evw[:, 0:512].indirect(T.roff[:, 0:8]), T.ev2[:, :]), a_roff, a_ev2, a_w0)
+    a_loff = v(lambda: V.tensor_copy(T.loff[:, :], T.l3[:, :]), t)
+    a_coff = v(lambda: V.tensor_scalar(T.coff[:, 0:3], T.zq[:, 0:3], 0.5, 63.5, A.mult, A.add), a_z)
+    w("y", a_ev)
+    for i in range(2):
+        Y.dma_start(T.ep[i:i + 1, :], T.evw[i:128:32, 0:64]).then_inc(sem.dev, 16)
+
+    cc, cs = pick(("kq", "kp"), (0, 64), ("lq", "ls"), (0, 128), "coff", (0, 4),
+                  (("aC", need["C"]), po[0], a_coff, a_c3), (("aS", need["S"]), po[1], a_coff, a_c3))
+    fin = []
+    for h in range(2):
+        fin.append(pick(("oq", "op"), (256 * h, 256 * h + 256), ("kq", "kp"), (0, 576), "loff", (16 * h, 16 * h + 16),
+                        (cc, a_loff), (cs, a_loff)))
+    yc = []
+    for h in range(2):
+        lo, hi = 256 * h, 256 * h + 256
+        ym = mm(lambda: E.matmul_mx(T.py[:, 512 * h:512 * h + 256], T.wq[:, :], T.ws[:, :], T.oq[:, lo:hi], T.op[:, lo:hi],
+                                    True, True), a_wq, *fin[h])
+        yc.append(v(lambda: V.tensor_copy(T.yb[:, lo:hi], T.py[:, 512 * h:512 * h + 256]), ym))
+    t = v(lambda: V.tensor_tensor(T.e1[0:2, :], T.ep[0:2, 0:128], T.ep[0:2, 128:256], A.add), ("dev", 32))
+    t = v(lambda: V.tensor_tensor(T.e2[0:2, :], T.e1[0:2, 0:64], T.e1[0:2, 64:128], A.add), t)
+    t = v(lambda: V.tensor_tensor(T.e3[0:2, :], T.e2[0:2, :], T.m64[0:2, :], A.mult), t, a_m64)
+    a_e4 = v(lambda: V.tensor_scalar(T.e4[0:2, :], T.e3[0:2, :], T.is0[0:2, 0:1], None, A.subtract), t)
+
+    outs = [0]
+
+    def store(nm, tag, o, i):
+        w(nm, tag)
+        queue[nm].dma_start(o, i).then_inc(sem.dout, 16)
+        outs[0] += 16
+
+    for h in range(2):
+        store("y", fin[h][0], T.oc[:, 1024 * h:1024 * h + 1024], u8(T.oq[:, 256 * h:256 * h + 256]))
+    for k in range(4):
+        store("s", fin[1][1], T.osc[4 * k:4 * k + 4, :], T.op[32 * k:32 * k + 4, :])
+    for h in range(2):
+        store("y", yc[h], T.y[:, 256 * h:256 * h + 256], T.yb[:, 256 * h:256 * h + 256])
+    store("s", a_e4, T.ev[:, :], T.e4[0:2, :])
+
+    w("g", ("sv", cnt["v"]), ("ss", cnt["s"]), ("st", cnt["t"]), ("sg", cnt["g"]), ("dout", outs[0]), ("loc", loc))

@@ -8,38 +8,43 @@ def _f32(n):
     return ("sbuf", [128, n], "float32")
 
 
-_I1 = ("sbuf", [128, 1], "int32")
+def _b16(n):
+    return ("sbuf", [128, n], "bfloat16")
+
+
+def _i32(n):
+    return ("sbuf", [128, n], "int32")
+
+
+def _u16(n):
+    return ("sbuf", [128, n], "uint16")
+
+
 SCRATCH = {
-    "snd": ("dram", [128, 1], "int32"), "snr": ("sbuf", [128, 8], "int32"), "xt": ("sbuf", [128, 520], "bfloat16"),
-    "ut": ("sbuf", [128, 512], "bfloat16"), "wt": ("sbuf", [128, 512], "bfloat16"),
-    "xq": ("sbuf", [128, 130], CODES), "xs": ("sbuf", [128, 130], PLANE),
+    "snd": ("dram", [128, 1], "int32"), "snr": _i32(8), "xt": _b16(512), "ut": _b16(512), "wt": _b16(512),
+    "xq": ("sbuf", [128, 128], CODES), "xs": ("sbuf", [128, 128], PLANE),
     "uq": ("sbuf", [128, 128], CODES), "us": ("sbuf", [128, 128], PLANE),
     "ur": ("sbuf", [128, 128], CODES), "urs": ("sbuf", [128, 128], PLANE),
     "wq": ("sbuf", [128, 128], CODES), "ws": ("sbuf", [128, 128], PLANE),
     "kq": ("sbuf", [128, 576], CODES), "kp": ("sbuf", [128, 576], PLANE),
     "pq": ("sbuf", [128, 128], CODES), "ps": ("sbuf", [128, 128], PLANE),
     "fwl": ("dram", [128, 1], "int32"), "fwq": ("sbuf", [128, 32], CODES), "fws": ("sbuf", [128, 32], PLANE),
-    "land": ("dram", [8, 128, 1], "int32"), "row": ("sbuf", [128, 1024], "int32"),
+    "land": ("dram", [8, 128, 1], "int32"), "row": _i32(1024), "rowb": _i32(128),
     "lq": ("sbuf", [128, 128], CODES), "ls": ("sbuf", [128, 128], PLANE),
     "oq": ("sbuf", [128, 512], CODES), "op": ("sbuf", [128, 512], PLANE),
-    "lst": ("sbuf", [128, 8], "uint16"), "lo": ("sbuf", [128, 2], "uint16"),
-    "zo": ("sbuf", [128, 8], "uint16"), "coff": ("sbuf", [128, 4], "uint16"),
-    "loff": ("sbuf", [128, 32], "uint16"), "roff": ("sbuf", [128, 16], "uint16"),
-    "qall": ("sbuf", [128, 2], "uint16"), "qown": ("sbuf", [128, 2], "uint16"),
-    "pi": _I1, "pm": _I1, "pm32": _I1, "ia": _I1, "ib": _I1, "ic": _I1, "id5": _I1,
-    "pmf": _f32(1), "fa": _f32(1), "fx": _f32(1), "fc": _f32(1), "fd": _f32(1), "is0": _f32(1), "nm": _f32(1),
-    "q16": _f32(32), "jw": _f32(32), "kb": _f32(4), "zr": _f32(128), "k64": _f32(64), "jio": _f32(128), "jrow": _f32(128),
-    "c0": ("sbuf", [128, 640], "bfloat16"), "c1": ("sbuf", [128, 640], "bfloat16"),
-    "c2": ("sbuf", [128, 640], "bfloat16"), "c3": ("sbuf", [128, 640], "bfloat16"),
-    "junk": ("sbuf", [128, 640], "bfloat16"), "junv": ("sbuf", [128, 128], "bfloat16"),
-    "tb": _f32(448), "tt": _f32(128), "rin": _f32(32), "rwp": _f32(32), "l1": _f32(32), "l2": _f32(32), "l3": _f32(32),
-    "fl": _f32(128), "pin1": _f32(128), "pinc": _f32(128), "zq": _f32(4), "zv": _f32(4), "m64": _f32(64),
-    "evi": _f32(128), "ev2": _f32(128), "evw": _f32(512), "ep": _f32(256), "e1": _f32(128), "e2": _f32(64), "e3": _f32(64),
-    "e4": _f32(64), "yb": _f32(512),
-    "pr": ("psum", [128, 512], "float32"), "pc": ("psum", [128, 2048], "float32"),
-    "p2": ("psum", [128, 512], "float32"), "py": ("psum", [128, 1024], "float32"),
+    "lst": _u16(8), "lo": _u16(2), "zo": _u16(8), "coff": _u16(4), "loff": _u16(32), "roff": _u16(16),
+    "qall": _u16(2), "qown": _u16(2), "gl": _u16(4),
+    "pf": _f32(1), "pw": _i32(8), "xa": _i32(2), "xb": _i32(2), "bt": _i32(8), "bs": _i32(4), "pm": _i32(1), "pmf": _f32(1),
+    "pj": _f32(1), "qs": _f32(2), "q64": _f32(32), "jw": _f32(32), "kb": _f32(4), "tri": _b16(128), "ntri": _b16(128),
+    "col": _f32(128), "colt": _f32(128),
+    "c0": _b16(256), "c1": _b16(256), "c2": _b16(512), "c3": _b16(512), "zd": _b16(512), "zz": _b16(512), "zj": _b16(512),
+    "part": _f32(2), "so": _b16(1024), "mm": _b16(32), "mt": _b16(32), "mg": _b16(64), "rr": _b16(64),
+    "l1": _f32(32), "l2": _f32(32), "l3": _f32(32),
+    "fl": _b16(128), "pinc": _b16(128), "zq": _f32(4), "junk": _b16(384), "junv": _b16(128), "junw": _b16(64),
+    "evw": _f32(576), "e1": _f32(64), "e2": _f32(64), "yb": _f32(512),
+    "pc": ("psum", [128, 2048], "float32"), "ra": ("psum", [128, 1024], "float32"), "rb": ("psum", [128, 1024], "float32"),
 }
-SEMAPHORES = ["sv", "ss", "st", "sg", "dsn", "dsd", "dx", "du", "dk", "dw", "down", "drow", "dr", "dev", "dout",
+SEMAPHORES = ["sv", "ss", "st", "sg", "dsn", "dsd", "dx", "du", "dka", "dkb", "dw", "down", "drow", "dout",
               "aL", "aC", "aS", "fC", "fS", "loc"]
 
 
@@ -166,6 +171,20 @@ def rank_program(g, core, T, topo):
     def gg(call, *tags):
         return do("g", call, tags)
 
+    def ts(out, in0, s1, op0, s2=None, op1=None, tags=()):
+        if op1 is None:
+            return v(lambda: V.tensor_scalar(out, in0, s1, None, op0), *tags)
+        return v(lambda: V.tensor_scalar(out, in0, s1, s2, op0, op1), *tags)
+
+    def tt(out, in0, in1, op, *tags):
+        return v(lambda: V.tensor_tensor(out, in0, in1, op), *tags)
+
+    def cp(out, in_, *tags):
+        return v(lambda: V.tensor_copy(out, in_), *tags)
+
+    def act(out, in_, func, *tags, **kw):
+        return sc(lambda: S.activation(out, in_, func, **kw), *tags)
+
     need = {"L": n - 1, "C": 0, "S": 0}
     for s in range(n):
         if s == r:
@@ -179,50 +198,56 @@ def rank_program(g, core, T, topo):
                 need[k] += len(es)
 
     Y.dma_start(T.snd[:, :], T.sn[:, :]).then_inc(sem.dsd, 16)
-    S.dma_start(T.xt[:, 8:520], T.x[:, :]).then_inc(sem.dx, 16)
+    S.dma_start(T.xt[:, :], T.x[:, :]).then_inc(sem.dx, 16)
+    Y.dma_start(T.ut[:, 0:8], T.u[:, 0:8]).then_inc(sem.du, 16)
     for k in range(8):
         (Y if k < 4 else S).dma_start(T.snr[16 * k:16 * k + 16, :], T.sn[:, :]).then_inc(sem.dsn, 16)
-    Y.dma_start(T.ut[:, 0:8], T.u[:, 0:8]).then_inc(sem.du, 16)
-    S.dma_start(T.kp[:, 64:576], T.ks[:, :]).then_inc(sem.dk, 16)
-    Y.dma_start(u8(T.kq[:, 64:576]), T.kc[:, :]).then_inc(sem.dk, 16)
-    Y.dma_start(T.wt[:, :], T.w[:, :]).then_inc(sem.dw, 16)
+    S.dma_start(T.kp[:, 64:576], T.ks[:, :]).then_inc(sem.dka, 16)
+    Y.dma_start(u8(T.kq[:, 64:320]), T.kc[:, 0:1024]).then_inc(sem.dka, 16)
+    Y.dma_start(u8(T.kq[:, 320:576]), T.kc[:, 1024:2048]).then_inc(sem.dkb, 16)
     Y.dma_start(T.land[r], T.sn[:, :]).then_inc(sem.down, 16)
-    SN, DX, DU, DK, DW = ("dsn", 128), ("dx", 16), ("du", 16), ("dk", 32), ("dw", 16)
+    SN, DX, DU, DKA, DKB, DW = ("dsn", 128), ("dx", 16), ("du", 16), ("dka", 32), ("dkb", 16), ("dw", 16)
 
-    a_x0 = v(lambda: V.memset(T.xt[:, 0:8], 0.0))
+    a_pf = gg(lambda: g.iota(T.pf[:, :], [[1, 1]], 0, 1, allow_small_or_imprecise_dtypes=True))
+    a_q = gg(lambda: g.iota(T.q64[:, :], [[16, 32]], 0, 0, allow_small_or_imprecise_dtypes=True))
+    a_tri = gg(lambda: g.iota(T.tri[:, :], [[1, 128]], 0, -1, allow_small_or_imprecise_dtypes=True))
     a_u0 = v(lambda: V.memset(T.ut[:, 8:512], 0.0))
     a_zo = v(lambda: V.memset(T.zo[:, :], 0))
-    a_pi = gg(lambda: g.iota(T.pi[:, :], [[1, 1]], 0, 1))
-    a_q16 = gg(lambda: g.iota(T.q16[:, :], [[16, 32]], 0, 0, allow_small_or_imprecise_dtypes=True))
-    a_jio = gg(lambda: g.iota(T.jio[:, :], [[1, 128]], 1, 4, allow_small_or_imprecise_dtypes=True))
-    t1 = v(lambda: V.tensor_scalar(T.ia[:, :], T.pi[:, :], 1, 3, A.logical_shift_right, A.bitwise_and), a_pi)
-    t2 = v(lambda: V.tensor_scalar(T.ib[:, :], T.pi[:, :], 1, None, A.bitwise_and))
-    t3 = v(lambda: V.tensor_scalar(T.ic[:, :], T.pi[:, :], 3, 1, A.logical_shift_right, A.bitwise_and))
-    t4 = v(lambda: V.tensor_scalar(T.id5[:, :], T.pi[:, :], 5, None, A.logical_shift_right))
-    t1 = v(lambda: V.tensor_scalar(T.fa[:, :], T.ia[:, :], 8, None, A.mult), t1)
-    t3 = v(lambda: V.tensor_scalar(T.fc[:, :], T.ic[:, :], 2, None, A.mult), t3)
-    t5 = v(lambda: V.tensor_scalar(T.pm32[:, :], T.pi[:, :], 31, None, A.bitwise_and))
-
-    cx, hm = P["cross"], P["home"]
-    stx, sth = cx[1] - cx[0], hm[1] - hm[0]
-    a_lx = v(lambda: V.tensor_scalar(T.lst[:, 0:4], T.snr[:, cx[0]:cx[0] + 3 * stx + 1:stx], 2, None, A.add), SN)
-    a_ly = v(lambda: V.tensor_scalar(T.lst[:, 4:8], T.snr[:, hm[0]:hm[0] + 3 * sth + 1:sth], 2, None, A.add))
-    a_lo = v(lambda: V.tensor_scalar(T.lo[:, 0:1], T.snr[:, r:r + 1], 2, None, A.add))
-    a_xq = v(lambda: V.quantize_mx(T.xq[:, 0:130], T.xs[:, 0:130], T.xt[:, 0:520]), DX, a_x0)
+    a_c0 = v(lambda: V.memset(T.col[:, :], 0.0))
+    a_w0 = v(lambda: V.memset(T.evw[:, 0:64], 0.0))
+    a_m0 = v(lambda: V.memset(T.mm[:, :], 0.0))
+    a_pw = ts(T.pw[:, :], T.q64[:, 0:8], 16.0, A.add, T.pf[:, 0:1], A.mult, (a_pf, a_q))
+    t = ts(T.pm[:, :], T.pw[:, 0:1], 4, A.logical_shift_right, 15, A.bitwise_and, (a_pw,))
+    t1 = ts(T.xa[:, :], T.pw[:, 0:2], 0x440, A.bitwise_and)
+    a_pm = ts(T.pmf[:, :], T.pm[:, :], 64.0, A.add, tags=(t,))
+    a_xb = ts(T.xb[:, :], T.xa[:, :], 17, A.mult, tags=(t1,))
+    t = act(T.pj[:, :], T.pf[:, :], F.Identity, a_pf, bias=0.75)
+    for a in range(4):
+        a_w1 = act(T.evw[32 * a:32 * a + 1, 0:64], T.evw[32 * a:32 * a + 1, 0:64], F.Identity, a_w0, bias=-0.25)
+    a_cj = act(T.col[:, 0:128:32], T.q64[:, 0:4], F.Identity, t, a_q, a_c0, bias=T.pj[:, 0:1], scale=8.0)
 
     def pick(o, oc, i, ic, off, lc, vt, st):
         x = v(lambda: V.tensor_copy(u32(T[o[0]][:, oc[0]:oc[1]]), u32(T[i[0]][:, ic[0]:ic[1]]).indirect(T[off][:, lc[0]:lc[1]])), *vt)
         y = sc(lambda: S.activation(T[o[1]][:, oc[0]:oc[1]], T[i[1]][:, ic[0]:ic[1]].indirect(T[off][:, lc[0]:lc[1]]), F.Copy), *st)
         return x, y
 
-    X, XW = ("xq", "xs"), (0, 130)
+    a_uq = v(lambda: V.quantize_mx(T.uq[:, :], T.us[:, :], T.ut[:, :]), DU, a_u0)
+    cx, hm = P["cross"], P["home"]
+    stx, sth = cx[1] - cx[0], hm[1] - hm[0]
+    a_lx = cp(T.lst[:, 0:4], T.snr[:, cx[0]:cx[0] + 3 * stx + 1:stx], SN)
+    a_ly = cp(T.lst[:, 4:8], T.snr[:, hm[0]:hm[0] + 3 * sth + 1:sth])
+    a_lo = cp(T.lo[:, 0:1], T.snr[:, r:r + 1])
+    ur = pick(("ur", "urs"), (0, 128), ("uq", "us"), (0, 128), "zo", (0, 8), (a_uq, a_zo), (a_uq, a_zo))
+    a_xq = v(lambda: V.quantize_mx(T.xq[:, :], T.xs[:, :], T.xt[:, :]), DX)
+    X, XW = ("xq", "xs"), (0, 128)
     px = pick(("pq", "ps"), (0, 64), X, XW, "lst", (0, 4), (a_xq, a_lx), (a_xq, a_lx))
     py = pick(("pq", "ps"), (64, 128), X, XW, "lst", (4, 8), (a_ly,), (a_ly,))
+    po = pick(("lq", "ls"), (16 * r, 16 * r + 16), X, XW, "lo", (0, 1), (a_lo,), (a_lo,))
 
     loc = 0
 
-    def send(ts, es):
-        g.remote_dma_fused(ts, local_sem=sem.loc)
+    def send(tr, es):
+        g.remote_dma_fused(tr, local_sem=sem.loc)
         return sum(len(e) for e in es)
 
     def hop(k):
@@ -249,87 +274,99 @@ def rank_program(g, core, T, topo):
     w("g", py[1])
     loc += straight("S")
 
-    a_uq = v(lambda: V.quantize_mx(T.uq[:, :], T.us[:, :], T.ut[:, :]), DU, a_u0)
-    ur = pick(("ur", "urs"), (0, 128), ("uq", "us"), (0, 128), "zo", (0, 8), (a_uq, a_zo), (a_uq, a_zo))
-    po = pick(("lq", "ls"), (16 * r, 16 * r + 16), X, XW, "lo", (0, 1), (a_lo,), (a_lo,))
-    a_row = mm(lambda: E.matmul_mx(T.pr[:, :], T.ur[:, :], T.urs[:, :], T.kq[:, 64:576], T.kp[:, 64:576], True, True), DK, *ur)
-    turn = (1, 2, 3, 0)
-    a_col = {}
-    for c in turn:
-        lo, hi = 64 + 128 * c, 192 + 128 * c
-        a_col[c] = mm(lambda: E.matmul_mx(T.pc[:, 512 * c:512 * c + 128], T.kq[:, lo:hi], T.kp[:, lo:hi],
-                                          T.ur[:, :], T.urs[:, :], True, True))
-    a_row2 = mm(lambda: E.matmul_mx(T.p2[:, :], T.ur[:, :], T.urs[:, :], T.kq[:, 64:576], T.kp[:, 64:576], True, True))
-    a_tin = v(lambda: V.memset(T.tb[:, 320:448], 0.0))
-    t1 = v(lambda: V.tensor_tensor(T.fx[:, :], T.fa[:, :], T.ib[:, :], A.add), t1, t2)
-    t = v(lambda: V.tensor_scalar(T.pm[:, :], T.pi[:, :], 15, None, A.bitwise_and))
-    t4 = v(lambda: V.tensor_scalar(T.fd[:, :], T.id5[:, :], 2, None, A.mult), t4)
-    a_pm = v(lambda: V.tensor_scalar(T.qall[:, 0:1], T.fx[:, :], T.fc[:, 0:1], None, A.add), t1, t3)
-    a_pm = v(lambda: V.tensor_scalar(T.qall[:, 1:2], T.fx[:, :], T.fc[:, 0:1], 4.0, A.add, A.add))
-    t = v(lambda: V.tensor_copy(T.pmf[:, :], T.pm[:, :]), t)
-    a_pq = v(lambda: V.tensor_scalar(T.qown[:, 0:1], T.fx[:, :], T.fd[:, 0:1], None, A.add), t4)
-    a_nm = v(lambda: V.tensor_scalar(T.nm[:, :], T.pm32[:, :], 0, None, A.is_gt), t5)
-    a_is0 = v(lambda: V.tensor_scalar(T.is0[:, :], T.pm32[:, :], 0, None, A.is_equal))
+    a_nt = ts(T.ntri[:, :], T.tri[:, :], 0.0, A.is_ge, 0.5, A.subtract, (a_tri,))
+    for i, (src, sh, mask) in enumerate(((T.xb[:, 0:1], 8, 4), (T.pw[:, 0:1], 7, 1), (T.pw[:, 3:4], 4, 24),
+                                         (T.xb[:, 1:2], 7, 8), (T.pw[:, 1:2], 0, 32), (T.pw[:, 0:1], 8, 6))):
+        t = ts(T.bt[:, i:i + 1], src, sh, A.logical_shift_right, mask, A.bitwise_and, (a_xb,))
+    t1 = ts(T.bs[:, 3:4], T.pw[:, 7:8], 7, A.logical_shift_right, 1, A.bitwise_and)
+    t = tt(T.bs[:, 0:3], T.bt[:, 0:3], T.bt[:, 3:6], A.add, t)
+    for k in range(2):
+        a_gl = ts(T.gl[:, k:4:2], T.q64[:, 0:2], -64.0, A.add, T.pmf[:, 0:1], A.add, (a_pm,))
+    a_qs = tt(T.qs[:, :], T.bs[:, 0:4:2], T.bs[:, 1:4:2], A.add, t, t1)
+    a_jw = act(T.jw[:, :], T.q64[:, :], F.Identity, a_pm, bias=T.pmf[:, 0:1])
+    a_kb = act(T.kb[:, :], T.jw[:, 0:4], F.Identity, a_jw, bias=-63.5)
 
-    sums = []
-    for c in turn:
+    def scores(h, rows, *tags):
+        lo = 64 + 256 * h
+        for c in range(2):
+            a = mm(lambda: E.matmul_mx(T.pc[:, 512 * (2 * h + c):512 * (2 * h + c) + 128], T.kq[:, lo + 128 * c:lo + 128 * c + 128],
+                                       T.kp[:, lo + 128 * c:lo + 128 * c + 128], T.uq[:, :], T.us[:, :], True, True), *tags)
+        b = [mm(lambda: E.matmul_mx(rows[:, 512 * k:512 * k + 256], T.ur[:, :], T.urs[:, :], T.kq[:, lo:lo + 256],
+                                    T.kp[:, lo:lo + 256], True, True), *ur) for k in range(2)]
+        return a, b[0], b[1]
+
+    ca, ras, rav = scores(0, T.ra, DKA, a_uq)
+    cb, rbs, rbv = scores(1, T.rb, DKB)
+
+    def sj(c):
+        return T.col[:, 32 * c + 1:32 * c + 2]
+
+    sa = act(T.col[:, 1:64:32], T.pc[:, 0:1024:512], F.Copy, ca, a_cj)
+    z = {}
+    for c in (0, 1):
+        z[c] = act(T.zd[:, 128 * c:128 * c + 128], T.ra[:, 128 * c:128 * c + 128], F.Sign, sa, ras, bias=sj(c), scale=-1.0)
+    sb = act(T.col[:, 65:128:32], T.pc[:, 1024:2048:512], F.Copy, cb)
+    S.dma_start(T.wt[:, :], T.w[:, :]).then_inc(sem.dw, 16)
+    for c in (2, 3):
+        z[c] = act(T.zd[:, 128 * c:128 * c + 128], T.rb[:, 128 * c - 256:128 * c - 128], F.Sign, sb, rbs, bias=sj(c), scale=-1.0)
+    zz = [act(T.zz[:, 256 * c:256 * c + 256], T.rb[:, 0:256], F.Sign, bias=sj(c), scale=-1.0) for c in (0, 1)]
+    pa = [act(T.zj[:, 256 * c:256 * c + 256], T.zz[:, 256 * c:256 * c + 256], F.Relu, zz[c], accum_out=T.part[:, c:c + 1])
+          for c in (0, 1)]
+
+    ts(T.c0[:, 128:256], T.ra[:, 640:768], sj(0), A.is_lt, tags=(sa, rav))
+    ts(T.c1[:, 128:256], T.ra[:, 512:640], sj(1), A.is_le)
+    tt(T.c0[:, 0:128], T.zd[:, 0:128], T.ntri[:, :], A.is_gt, z[0], a_nt)
+    d01 = tt(T.c1[:, 0:128], T.zd[:, 128:256], T.ntri[:, :], A.is_gt, z[1])
+    ts(T.c2[:, 0:256], T.ra[:, 512:768], sj(2), A.is_le, tags=(sb,))
+    ts(T.c3[:, 0:256], T.ra[:, 512:768], sj(3), A.is_le)
+    ts(T.c2[:, 384:512], T.rb[:, 640:768], sj(2), A.is_lt, tags=(rbv,))
+    ts(T.c3[:, 256:384], T.rb[:, 512:640], sj(3), A.is_le)
+    d2 = tt(T.c2[:, 256:384], T.zd[:, 256:384], T.ntri[:, :], A.is_gt, z[2])
+    d3 = tt(T.c3[:, 384:512], T.zd[:, 384:512], T.ntri[:, :], A.is_gt, z[3])
+
+    def total(c, k, first, *tags):
         b = T["c%d" % c]
-        sj = T.pc[:, 512 * c:512 * c + 1]
-        own = T.pr[:, 128 * c:128 * c + 128]
-        t0 = v(lambda: V.tensor_scalar(b[:, 512:640], own, sj, None, A.is_equal), a_row, a_col[c])
-        masked = gg(lambda: g.affine_select(b[:, 512:640], b[:, 512:640], [[-1, 128]], A.is_gt, 0.0, 0, 1), t0)
-        if c:
-            v(lambda: V.tensor_scalar(b[:, 0:128 * c], T.pr[:, 0:128 * c], sj, None, A.is_le))
-        t0 = v(lambda: V.tensor_scalar(b[:, 128 * c:512], T.pr[:, 128 * c:512], sj, None, A.is_lt))
-        if c:
-            sums.append(sc(lambda: S.activation(T.junk[:, :], b[:, :], F.Copy, accum_out=T.tb[:, 320 + 32 * c:321 + 32 * c]),
-                           t0, masked, a_tin, *sums[-1:]))
-        else:
-            sums.append(v(lambda: V.tensor_tensor_scan(T.tb[:, 1:321], b[:, 0:320], b[:, 320:640], 0.0, A.add, A.add),
-                          t0, masked, a_tin))
-    a_k64 = gg(lambda: g.iota(T.k64[:, :], [[1, 64]], 0, 0, allow_small_or_imprecise_dtypes=True))
+        return v(lambda: V.tensor_tensor_scan(T.so[:, 256 * c + 256 - k:256 * c + 256], b[:, 0:k], b[:, k:2 * k], first,
+                                              A.add, A.add), *tags)
+
+    total(2, 256, 0.0, d2)
+    total(3, 256, 0.0, d3)
+    a_qa = ts(T.qall[:, :], T.q64[:, 0:2], 0.125, A.mult, T.qs[:, 0:1], A.add, (a_qs,))
+    total(0, 128, T.part[:, 0:1], pa[0], d01)
+    a_so = total(1, 128, T.part[:, 1:2], pa[1])
+
+    cp(T.mm[0:64, 0:4], T.so[0:64, 255:1024:256], a_so, a_m0)
+    t = cp(T.mm[0:64, 4:8], T.so[64:128, 255:1024:256])
+    act(T.mm[64:128, 0:4], T.so[64:128, 255:1024:256], F.Copy, a_so, a_m0)
+    t1 = act(T.mm[64:128, 4:8], T.so[0:64, 255:1024:256], F.Copy)
+    cp(T.mm[0:32, 8:16], T.mm[32:64, 0:8], t)
+    t = cp(T.mm[32:64, 8:16], T.mm[0:32, 0:8])
+    act(T.mm[64:96, 8:16], T.mm[96:128, 0:8], F.Copy, t1)
+    t1 = act(T.mm[96:128, 8:16], T.mm[64:96, 0:8], F.Copy)
+    a_qo = cp(T.qown[:, 0:1], T.qs[:, 1:2])
+    t = v(lambda: V.transpose(T.mt[:, :], T.mm[:, :]), t, t1)
+    t = cp(T.mg[:, :], T.mt[:, :].indirect(T.gl[:, 0:4]), t, a_gl)
+    a_rr = v(lambda: V.transpose(T.rr[:, :], T.mg[:, :]), t)
+    a_wq = v(lambda: V.quantize_mx(T.wq[:, :], T.ws[:, :], T.wt[:, :]), DW)
+    a_ct = v(lambda: V.transpose(T.colt[:, :], T.col[:, :]), sb)
+
     w("y", ("aL", need["L"]), ("down", 16))
     Y.dma_start(T.row[0:1, :], T.land[:, :, :]).then_inc(sem.drow, 16)
-    a_tt = v(lambda: V.transpose(T.tt[:, :], T.tb[:, 320:448]), *sums)
-    for a in range(4):
-        nm = "sy"[a % 2]
-        w(nm, a_tt)
-        queue[nm].dma_start(T.rin[32 * a:32 * a + 32, 0:16], T.tt[0:128:32, :]).then_inc(sem.dr, 16)
-    a_kb = v(lambda: V.tensor_scalar(T.kb[:, :], T.q16[:, 0:4], T.pmf[:, 0:1], 0.5, A.add, A.add), t, a_q16)
-    a_jw = v(lambda: V.tensor_scalar(T.jw[:, :], T.q16[:, :], T.pmf[:, 0:1], 64.0, A.add, A.add))
-    a_zr = v(lambda: V.memset(T.zr[0:1, :], 0.0))
-    for a in range(4):
-        a_evi = sc(lambda: S.activation(T.evi[32 * a:32 * a + 32, :], T.p2[32 * a:32 * a + 32, 128 * a:128 * a + 128], F.Identity,
-                                        scale=T.nm[32 * a:32 * a + 32, 0:1]), a_row2, a_nm)
-    a_wq = v(lambda: V.quantize_mx(T.wq[:, :], T.ws[:, :], T.wt[:, :]), DW)
-
-    t = v(lambda: V.tensor_scalar(T.fl[0:1, :], T.row[0:1, r:1024:8], 0, None, A.is_ge), ("drow", 16))
-    t = v(lambda: V.tensor_tensor_scan(T.pin1[0:1, :], T.fl[0:1, :], T.zr[0:1, :], 0.0, A.add, A.add), t, a_zr)
-    a_pinc = gg(lambda: g.partition_broadcast(T.pinc[:, :], T.pin1[0:1, :], 128), t)
+    a_b = gg(lambda: g.partition_broadcast(T.rowb[:, :], T.row[0:1, r:1024:8], 128), ("drow", 16))
+    t = ts(T.fl[:, :], T.rowb[:, :], 0, A.is_ge, tags=(a_b,))
+    a_pinc = v(lambda: V.tensor_tensor_scan(T.pinc[:, :], T.fl[:, :], T.fl[:, :], 0.0, A.add, A.max), t)
     m = T.pinc[:, 127:128]
-    a_z = sums[2]
     for q in range(3):
-        a_z = sc(lambda: S.activation(T.junk[:, 0:127], T.pinc[:, 0:127], F.Sign, bias=T.kb[:, q:q + 1], scale=-1.0,
-                                      accum_out=T.zq[:, q:q + 1]), a_pinc, a_kb, a_z)
-    a_jr = v(lambda: V.tensor_scalar(T.jrow[:, :], T.jio[:, :], T.is0[:, 0:1], None, A.mult), a_jio, a_is0)
-    a_w0 = v(lambda: V.memset(T.evw[:, 0:64], 0.0))
-    a_ev2 = v(lambda: V.tensor_tensor(T.ev2[:, :], T.evi[:, :], T.jrow[:, :], A.add), a_evi, a_jr)
-    t1 = v(lambda: V.tensor_scalar(T.junv[:, 0:127], T.pinc[:, 0:127], T.kb[:, 3:4], None, A.is_le), a_pinc)
-    a_m64 = v(lambda: V.tensor_scalar(T.m64[0:2, :], T.k64[0:2, :], T.pinc[0:2, 127:128], None, A.is_lt), a_k64)
-    t1 = v(lambda: V.tensor_reduce(T.zv[:, 0:1], T.junv[:, 0:127], AX.X, A.add), t1)
-    t = v(lambda: V.tensor_copy(T.rin[:, 16:32], T.rin[:, 0:16]), ("dr", 64))
-    a_c3 = v(lambda: V.tensor_copy(T.coff[:, 3:4], T.zv[:, 0:1]), t1)
-    a_rwp = v(lambda: V.transpose(T.rwp[:, :], T.rin[:, :]), t)
-    t = v(lambda: V.tensor_scalar(T.l1[:, :], T.rwp[:, :].indirect(T.qall[:, 0:2]), m, 2048.0, A.is_ge, A.mult), a_rwp, a_pm)
-    a_roff = v(lambda: V.tensor_copy(T.roff[:, :], T.rwp[:, :].indirect(T.qown[:, 0:1])), a_pq)
-    t = v(lambda: V.tensor_tensor(T.l2[:, :], T.rwp[:, :].indirect(T.qall[:, 0:2]), T.l1[:, :], A.max), t)
-    t = v(lambda: V.tensor_tensor(T.l3[:, :], T.l2[:, :], T.jw[:, :], A.min), t, a_jw)
-    a_ev = v(lambda: V.tensor_copy(T.evw[:, 0:512].indirect(T.roff[:, 0:8]), T.ev2[:, :]), a_roff, a_ev2, a_w0)
-    a_loff = v(lambda: V.tensor_copy(T.loff[:, :], T.l3[:, :]), t)
-    a_coff = v(lambda: V.tensor_scalar(T.coff[:, 0:3], T.zq[:, 0:3], 0.5, 63.5, A.mult, A.add), a_z)
-    w("y", a_ev)
-    for i in range(2):
-        Y.dma_start(T.ep[i:i + 1, :], T.evw[i:128:32, 0:64]).then_inc(sem.dev, 16)
+        a_z = act(T.junk[:, 128 * q:128 * q + 127], T.pinc[:, 0:127], F.Sign, a_pinc, a_kb, bias=T.kb[:, q:q + 1], scale=-1.0,
+                  accum_out=T.zq[:, q:q + 1])
+    t1 = ts(T.junv[:, :], T.pinc[:, :], T.kb[:, 3:4], A.is_le, tags=(a_pinc, a_kb))
+    t = ts(T.l1[:, :], T.rr[:, :].indirect(T.qall[:, 0:2]), m, A.is_ge, 2048.0, A.mult, (a_rr, a_qa))
+    t1 = v(lambda: V.tensor_tensor_scan(T.junw[:, :], T.junv[:, 0:64], T.junv[:, 64:128], 0.0, A.add, A.add), t1)
+    t = tt(T.l2[:, :], T.rr[:, :].indirect(T.qall[:, 0:2]), T.l1[:, :], A.max, t)
+    a_c3 = ts(T.coff[:, 3:4], T.junw[:, 63:64], 127.0, A.min, tags=(t1,))
+    a_l3 = tt(T.l3[:, :], T.l2[:, :], T.jw[:, :], A.min, t, a_jw)
+    a_loff = cp(T.loff[:, :], T.l3[:, :], a_l3)
+    a_coff = ts(T.coff[:, 0:3], T.zq[:, 0:3], 0.5, A.mult, 63.5, A.add, (a_z,))
 
     cc, cs = pick(("kq", "kp"), (0, 64), ("lq", "ls"), (0, 128), "coff", (0, 4),
                   (("aC", need["C"]), po[0], a_coff, a_c3), (("aS", need["S"]), po[1], a_coff, a_c3))
@@ -340,13 +377,13 @@ def rank_program(g, core, T, topo):
     yc = []
     for h in range(2):
         lo, hi = 256 * h, 256 * h + 256
-        ym = mm(lambda: E.matmul_mx(T.py[:, 512 * h:512 * h + 256], T.wq[:, :], T.ws[:, :], T.oq[:, lo:hi], T.op[:, lo:hi],
+        ym = mm(lambda: E.matmul_mx(T.pc[:, 512 * h:512 * h + 256], T.wq[:, :], T.ws[:, :], T.oq[:, lo:hi], T.op[:, lo:hi],
                                     True, True), a_wq, *fin[h])
-        yc.append(v(lambda: V.tensor_copy(T.yb[:, lo:hi], T.py[:, 512 * h:512 * h + 256]), ym))
-    t = v(lambda: V.tensor_tensor(T.e1[0:2, :], T.ep[0:2, 0:128], T.ep[0:2, 128:256], A.add), ("dev", 32))
-    t = v(lambda: V.tensor_tensor(T.e2[0:2, :], T.e1[0:2, 0:64], T.e1[0:2, 64:128], A.add), t)
-    t = v(lambda: V.tensor_tensor(T.e3[0:2, :], T.e2[0:2, :], T.m64[0:2, :], A.mult), t, a_m64)
-    a_e4 = v(lambda: V.tensor_scalar(T.e4[0:2, :], T.e3[0:2, :], T.is0[0:2, 0:1], None, A.subtract), t)
+        yc.append(act(T.yb[:, lo:hi], T.pc[:, 512 * h:512 * h + 256], F.Copy, ym))
+    t = cp(T.roff[:, :], T.l3[:, :].indirect(T.qown[:, 0:1]), a_qo)
+    t = cp(T.evw[:, 0:576].indirect(T.roff[:, 0:8]), T.colt[:, :], t, a_ct, a_w1)
+    t = tt(T.e1[0:64, :], T.evw[0:64, 0:64], T.evw[64:128, 0:64], A.add, t)
+    a_ev = tt(T.e2[0:32, :], T.e1[0:32, :], T.e1[32:64, :], A.add, t)
 
     outs = [0]
 
@@ -357,10 +394,10 @@ def rank_program(g, core, T, topo):
 
     for h in range(2):
         store("y", fin[h][0], T.oc[:, 1024 * h:1024 * h + 1024], u8(T.oq[:, 256 * h:256 * h + 256]))
-    for k in range(4):
-        store("s", fin[1][1], T.osc[4 * k:4 * k + 4, :], T.op[32 * k:32 * k + 4, :])
     for h in range(2):
         store("y", yc[h], T.y[:, 256 * h:256 * h + 256], T.yb[:, 256 * h:256 * h + 256])
-    store("s", a_e4, T.ev[:, :], T.e4[0:2, :])
+    for k in range(4):
+        store("s", fin[1][1], T.osc[4 * k:4 * k + 4, :], T.op[32 * k:32 * k + 4, :])
+    store("y", a_ev, T.ev[:, :], T.e2[0:2, :])
 
     w("g", ("sv", cnt["v"]), ("ss", cnt["s"]), ("st", cnt["t"]), ("sg", cnt["g"]), ("dout", outs[0]), ("loc", loc))

@@ -35,12 +35,12 @@ SCRATCH = {
     "lst": _u16(8), "lo": _u16(2), "zo": _u16(8), "coff": _u16(4), "loff": _u16(32), "roff": _u16(16),
     "qall": _u16(2), "qown": _u16(2), "gl": _u16(4),
     "pf": _f32(1), "pw": _i32(8), "xa": _i32(2), "xb": _i32(2), "bt": _i32(8), "bs": _i32(4), "pm": _i32(1), "pmf": _f32(1),
-    "pj": _f32(1), "qs": _f32(2), "q64": _f32(32), "jw": _f32(32), "kb": _f32(4), "tri": _b16(128), "ntri": _b16(128),
+    "pj": _f32(1), "qs": _f32(2), "q64": _f32(32), "jw": _f32(64), "kb": _f32(4), "tri": _b16(128), "ntri": _b16(128),
     "col": _f32(128), "colt": _f32(128),
     "c0": _b16(256), "c1": _b16(256), "c2": _b16(512), "c3": _b16(512), "zd": _b16(512), "zz": _b16(512), "zj": _b16(512),
-    "part": _f32(2), "so": _b16(1024), "mm": _b16(32), "mt": _b16(32), "mg": _b16(64), "rr": _b16(64),
-    "l1": _f32(32), "l2": _f32(32), "l3": _f32(32),
-    "fl": _b16(128), "pinc": _b16(128), "zq": _f32(4), "junk": _b16(384), "junv": _b16(128), "junw": _b16(64),
+    "part": _f32(2), "so": _b16(1056), "mt": _b16(32), "mg": _b16(64), "rr": _b16(64),
+    "l1": _f32(32), "l2": _f32(64), "l3": _f32(64),
+    "fl": _b16(128), "pinc": _b16(128), "zq": _f32(256), "junk": _b16(384), "junv": _b16(128),
     "evw": _f32(576), "e1": _f32(64), "e2": _f32(64), "yb": _f32(512),
     "pc": ("psum", [128, 2048], "float32"), "ra": ("psum", [128, 1024], "float32"), "rb": ("psum", [128, 1024], "float32"),
 }
@@ -214,16 +214,20 @@ def rank_program(g, core, T, topo):
     a_u0 = v(lambda: V.memset(T.ut[:, 8:512], 0.0))
     a_zo = v(lambda: V.memset(T.zo[:, :], 0))
     a_c0 = v(lambda: V.memset(T.col[:, :], 0.0))
-    a_w0 = v(lambda: V.memset(T.evw[:, 0:64], 0.0))
-    a_m0 = v(lambda: V.memset(T.mm[:, :], 0.0))
     a_pw = ts(T.pw[:, :], T.q64[:, 0:8], 16.0, A.add, T.pf[:, 0:1], A.mult, (a_pf, a_q))
     t = ts(T.pm[:, :], T.pw[:, 0:1], 4, A.logical_shift_right, 15, A.bitwise_and, (a_pw,))
     t1 = ts(T.xa[:, :], T.pw[:, 0:2], 0x440, A.bitwise_and)
     a_pm = ts(T.pmf[:, :], T.pm[:, :], 64.0, A.add, tags=(t,))
     a_xb = ts(T.xb[:, :], T.xa[:, :], 17, A.mult, tags=(t1,))
+    pieces = [(T.bt[:, 0:1], T.xb[:, 0:1], 8, 4), (T.bt[:, 1:2], T.pw[:, 0:1], 7, 1), (T.bt[:, 2:3], T.pw[:, 3:4], 3, 48),
+              (T.bt[:, 3:4], T.xb[:, 1:2], 7, 8), (T.bt[:, 4:5], T.pw[:, 1:2], 0, 32), (T.bt[:, 5:6], T.pw[:, 0:1], 7, 12),
+              (T.bs[:, 3:4], T.pw[:, 1:2], 4, 2)]
+
+    def piece():
+        o, src, sh, mask = pieces.pop()
+        return ts(o, src, sh, A.logical_shift_right, mask, A.bitwise_and, (a_xb,))
+
     t = act(T.pj[:, :], T.pf[:, :], F.Identity, a_pf, bias=0.75)
-    for a in range(4):
-        a_w1 = act(T.evw[32 * a:32 * a + 1, 0:64], T.evw[32 * a:32 * a + 1, 0:64], F.Identity, a_w0, bias=-0.25)
     a_cj = act(T.col[:, 0:128:32], T.q64[:, 0:4], F.Identity, t, a_q, a_c0, bias=T.pj[:, 0:1], scale=8.0)
 
     def pick(o, oc, i, ic, off, lc, vt, st):
@@ -239,6 +243,8 @@ def rank_program(g, core, T, topo):
     a_lo = cp(T.lo[:, 0:1], T.snr[:, r:r + 1])
     ur = pick(("ur", "urs"), (0, 128), ("uq", "us"), (0, 128), "zo", (0, 8), (a_uq, a_zo), (a_uq, a_zo))
     a_xq = v(lambda: V.quantize_mx(T.xq[:, :], T.xs[:, :], T.xt[:, :]), DX)
+    piece()
+    piece()
     X, XW = ("xq", "xs"), (0, 128)
     px = pick(("pq", "ps"), (0, 64), X, XW, "lst", (0, 4), (a_xq, a_lx), (a_xq, a_lx))
     py = pick(("pq", "ps"), (64, 128), X, XW, "lst", (4, 8), (a_ly,), (a_ly,))
@@ -275,16 +281,9 @@ def rank_program(g, core, T, topo):
     loc += straight("S")
 
     a_nt = ts(T.ntri[:, :], T.tri[:, :], 0.0, A.is_ge, 0.5, A.subtract, (a_tri,))
-    for i, (src, sh, mask) in enumerate(((T.xb[:, 0:1], 8, 4), (T.pw[:, 0:1], 7, 1), (T.pw[:, 3:4], 4, 24),
-                                         (T.xb[:, 1:2], 7, 8), (T.pw[:, 1:2], 0, 32), (T.pw[:, 0:1], 8, 6))):
-        t = ts(T.bt[:, i:i + 1], src, sh, A.logical_shift_right, mask, A.bitwise_and, (a_xb,))
-    t1 = ts(T.bs[:, 3:4], T.pw[:, 7:8], 7, A.logical_shift_right, 1, A.bitwise_and)
-    t = tt(T.bs[:, 0:3], T.bt[:, 0:3], T.bt[:, 3:6], A.add, t)
-    for k in range(2):
-        a_gl = ts(T.gl[:, k:4:2], T.q64[:, 0:2], -64.0, A.add, T.pmf[:, 0:1], A.add, (a_pm,))
-    a_qs = tt(T.qs[:, :], T.bs[:, 0:4:2], T.bs[:, 1:4:2], A.add, t, t1)
-    a_jw = act(T.jw[:, :], T.q64[:, :], F.Identity, a_pm, bias=T.pmf[:, 0:1])
-    a_kb = act(T.kb[:, :], T.jw[:, 0:4], F.Identity, a_jw, bias=-63.5)
+    a_m0 = v(lambda: V.memset(T.so[:, 1040:1056], 0.0))
+    piece()
+    piece()
 
     def scores(h, rows, *tags):
         lo = 64 + 256 * h
@@ -326,50 +325,66 @@ def rank_program(g, core, T, topo):
 
     def total(c, k, first, *tags):
         b = T["c%d" % c]
-        return v(lambda: V.tensor_tensor_scan(T.so[:, 256 * c + 256 - k:256 * c + 256], b[:, 0:k], b[:, k:2 * k], first,
+        return v(lambda: V.tensor_tensor_scan(T.so[:, 1028 - 4 * k + c:1028:4], b[:, 0:k], b[:, k:2 * k], first,
                                               A.add, A.add), *tags)
 
+    piece()
     total(2, 256, 0.0, d2)
     total(3, 256, 0.0, d3)
-    a_qa = ts(T.qall[:, :], T.q64[:, 0:2], 0.125, A.mult, T.qs[:, 0:1], A.add, (a_qs,))
     total(0, 128, T.part[:, 0:1], pa[0], d01)
     a_so = total(1, 128, T.part[:, 1:2], pa[1])
 
-    cp(T.mm[0:64, 0:4], T.so[0:64, 255:1024:256], a_so, a_m0)
-    t = cp(T.mm[0:64, 4:8], T.so[64:128, 255:1024:256])
-    act(T.mm[64:128, 0:4], T.so[64:128, 255:1024:256], F.Copy, a_so, a_m0)
-    t1 = act(T.mm[64:128, 4:8], T.so[0:64, 255:1024:256], F.Copy)
-    cp(T.mm[0:32, 8:16], T.mm[32:64, 0:8], t)
-    t = cp(T.mm[32:64, 8:16], T.mm[0:32, 0:8])
-    act(T.mm[64:96, 8:16], T.mm[96:128, 0:8], F.Copy, t1)
-    t1 = act(T.mm[96:128, 8:16], T.mm[64:96, 0:8], F.Copy)
-    a_qo = cp(T.qown[:, 0:1], T.qs[:, 1:2])
-    t = v(lambda: V.transpose(T.mt[:, :], T.mm[:, :]), t, t1)
+    def mp(p0, p1, c0, c1):
+        return T.so[p0:p1, 1024 + c0:1024 + c1]
+
+    piece()
+    a_bt = piece()
+    t = cp(mp(0, 64, 4, 8), mp(64, 128, 0, 4), a_so)
+    t1 = act(mp(64, 128, 4, 8), mp(0, 64, 0, 4), F.Copy, a_so)
+    for k in range(2):
+        a_gl = ts(T.gl[:, k:4:2], T.q64[:, 0:2], -64.0, A.add, T.pmf[:, 0:1], A.add, (a_pm,))
+    cp(mp(0, 32, 8, 16), mp(32, 64, 0, 8), t)
+    t = cp(mp(32, 64, 8, 16), mp(0, 32, 0, 8))
+    a_j0 = act(T.jw[:, 0:64:2], T.q64[:, :], F.Identity, scale=0.0)
+    act(mp(64, 96, 8, 16), mp(96, 128, 0, 8), F.Copy, t1)
+    t1 = act(mp(96, 128, 8, 16), mp(64, 96, 0, 8), F.Copy)
+    a_jw = act(T.jw[:, 1:64:2], T.q64[:, :], F.Identity, a_pm, bias=T.pmf[:, 0:1])
+    a_w0 = act(T.evw[:, 0:64], T.tri[:, 0:64], F.Identity, a_tri, scale=0.0)
+    a_kb = act(T.kb[:, :], T.jw[:, 1:8:2], F.Identity, a_jw, bias=-63.5)
+    for a in range(4):
+        a_w1 = act(T.evw[32 * a:32 * a + 1, 0:64], T.evw[32 * a:32 * a + 1, 0:64], F.Identity, a_w0, bias=-0.25)
+    t2 = tt(T.bs[:, 0:3], T.bt[:, 0:3], T.bt[:, 3:6], A.add, a_bt)
+    t = v(lambda: V.transpose(T.mt[:, :], mp(0, 128, 0, 32)), t, t1, a_m0)
+    a_qs = tt(T.qs[:, :], T.bs[:, 0:4:2], T.bs[:, 1:4:2], A.add, t2)
     t = cp(T.mg[:, :], T.mt[:, :].indirect(T.gl[:, 0:4]), t, a_gl)
+    a_qa = ts(T.qall[:, :], T.q64[:, 0:2], 0.125, A.mult, T.qs[:, 0:1], A.add, (a_qs,))
+    a_v0 = v(lambda: V.memset(T.junv[:, 127:128], 0.0))
     a_rr = v(lambda: V.transpose(T.rr[:, :], T.mg[:, :]), t)
     a_wq = v(lambda: V.quantize_mx(T.wq[:, :], T.ws[:, :], T.wt[:, :]), DW)
-    a_ct = v(lambda: V.transpose(T.colt[:, :], T.col[:, :]), sb)
+    a_l1 = ts(T.l1[:, :], T.rr[:, :].indirect(T.qall[:, 0:2]), 64.0, A.min, tags=(a_rr, a_qa))
+    ts(T.l2[:, 1:64:2], T.rr[:, :].indirect(T.qall[:, 0:2]), 64.0, A.min)
 
     w("y", ("aL", need["L"]), ("down", 16))
     Y.dma_start(T.row[0:1, :], T.land[:, :, :]).then_inc(sem.drow, 16)
     a_b = gg(lambda: g.partition_broadcast(T.rowb[:, :], T.row[0:1, r:1024:8], 128), ("drow", 16))
     t = ts(T.fl[:, :], T.rowb[:, :], 0, A.is_ge, tags=(a_b,))
+    a_qo = ts(T.qown[:, 0:1], T.qs[:, 1:2], 1.0, A.add)
     a_pinc = v(lambda: V.tensor_tensor_scan(T.pinc[:, :], T.fl[:, :], T.fl[:, :], 0.0, A.add, A.max), t)
+    a_ct = v(lambda: V.transpose(T.colt[:, :], T.col[:, :]), sb)
     m = T.pinc[:, 127:128]
     for q in range(3):
         a_z = act(T.junk[:, 128 * q:128 * q + 127], T.pinc[:, 0:127], F.Sign, a_pinc, a_kb, bias=T.kb[:, q:q + 1], scale=-1.0,
-                  accum_out=T.zq[:, q:q + 1])
-    t1 = ts(T.junv[:, :], T.pinc[:, :], T.kb[:, 3:4], A.is_le, tags=(a_pinc, a_kb))
-    t = ts(T.l1[:, :], T.rr[:, :].indirect(T.qall[:, 0:2]), m, A.is_ge, 2048.0, A.mult, (a_rr, a_qa))
-    t1 = v(lambda: V.tensor_tensor_scan(T.junw[:, :], T.junv[:, 0:64], T.junv[:, 64:128], 0.0, A.add, A.add), t1)
-    t = tt(T.l2[:, :], T.rr[:, :].indirect(T.qall[:, 0:2]), T.l1[:, :], A.max, t)
-    a_c3 = ts(T.coff[:, 3:4], T.junw[:, 63:64], 127.0, A.min, tags=(t1,))
-    a_l3 = tt(T.l3[:, :], T.l2[:, :], T.jw[:, :], A.min, t, a_jw)
-    a_loff = cp(T.loff[:, :], T.l3[:, :], a_l3)
-    a_coff = ts(T.coff[:, 0:3], T.zq[:, 0:3], 0.5, A.mult, 63.5, A.add, (a_z,))
+                  accum_out=T.zq[:, 64 * q + 63:64 * q + 64])
+    t = ts(T.l2[:, 0:64:2], T.l1[:, :], m, A.is_ge, tags=(a_pinc,))
+    t1 = ts(T.junv[:, 0:127], T.pinc[:, 0:127], T.kb[:, 3:4], A.is_le, 2.0, A.mult, (a_kb,))
+    t = v(lambda: V.tensor_tensor_scan(T.l3[:, :], T.jw[:, :], T.l2[:, :], 0.0, A.mult, A.max), t, a_jw)
+    t1 = v(lambda: V.tensor_tensor_scan(T.zq[:, 192:256], T.junv[:, 0:64], T.junv[:, 64:128], -127.0, A.add, A.add), t1)
+    a_loff = cp(T.loff[:, :], T.l3[:, 1:64:2], t)
+    a_roff = cp(T.roff[:, :], T.l3[:, :].indirect(T.qown[:, 0:1]))
+    a_coff = ts(T.coff[:, :], T.zq[:, 63:256:64], 0.5, A.mult, 63.5, A.add, (a_z, t1))
 
     cc, cs = pick(("kq", "kp"), (0, 64), ("lq", "ls"), (0, 128), "coff", (0, 4),
-                  (("aC", need["C"]), po[0], a_coff, a_c3), (("aS", need["S"]), po[1], a_coff, a_c3))
+                  (("aC", need["C"]), po[0], a_coff), (("aS", need["S"]), po[1], a_coff))
     fin = []
     for h in range(2):
         fin.append(pick(("oq", "op"), (256 * h, 256 * h + 256), ("kq", "kp"), (0, 576), "loff", (16 * h, 16 * h + 16),
@@ -380,8 +395,7 @@ def rank_program(g, core, T, topo):
         ym = mm(lambda: E.matmul_mx(T.pc[:, 512 * h:512 * h + 256], T.wq[:, :], T.ws[:, :], T.oq[:, lo:hi], T.op[:, lo:hi],
                                     True, True), a_wq, *fin[h])
         yc.append(act(T.yb[:, lo:hi], T.pc[:, 512 * h:512 * h + 256], F.Copy, ym))
-    t = cp(T.roff[:, :], T.l3[:, :].indirect(T.qown[:, 0:1]), a_qo)
-    t = cp(T.evw[:, 0:576].indirect(T.roff[:, 0:8]), T.colt[:, :], t, a_ct, a_w1)
+    t = cp(T.evw[:, :].indirect(T.roff[:, 0:8]), T.colt[:, :], a_roff, a_ct, a_w1)
     t = tt(T.e1[0:64, :], T.evw[0:64, 0:64], T.evw[64:128, 0:64], A.add, t)
     a_ev = tt(T.e2[0:32, :], T.e1[0:32, :], T.e1[32:64, :], A.add, t)
 
@@ -394,8 +408,8 @@ def rank_program(g, core, T, topo):
 
     for h in range(2):
         store("y", fin[h][0], T.oc[:, 1024 * h:1024 * h + 1024], u8(T.oq[:, 256 * h:256 * h + 256]))
-    for h in range(2):
-        store("y", yc[h], T.y[:, 256 * h:256 * h + 256], T.yb[:, 256 * h:256 * h + 256])
+    store("y", yc[0], T.y[:, 0:256], T.yb[:, 0:256])
+    store("y", yc[1], T.y[:, 256:512], T.yb[:, 256:512])
     for k in range(4):
         store("s", fin[1][1], T.osc[4 * k:4 * k + 4, :], T.op[32 * k:32 * k + 4, :])
     store("y", a_ev, T.ev[:, :], T.e2[0:2, :])

from concourse.bass import DstId, RemoteDMATransfer
from concourse.mybir import dt, AluOpType as A, AxisListType as AX, ActivationFunctionType as F

CODES, PLANE = "float8_e4m3fn_x4", "uint8"


def _f32(n):
    return ("sbuf", [128, n], "float32")


def _b16(n):
    return ("sbuf", [128, n], "bfloat16")


def _i32(n):
    return ("sbuf", [128, n], "int32")


def _u16(n):
    return ("sbuf", [128, n], "uint16")


SCRATCH = {
    "snd": ("dram", [128, 1], "int32"), "snr": _i32(8), "xt": _b16(512), "ut": _b16(512), "wt": _b16(512),
    "xq": ("sbuf", [128, 128], CODES), "xs": ("sbuf", [128, 128], PLANE),
    "uq": ("sbuf", [128, 128], CODES), "us": ("sbuf", [128, 128], PLANE),
    "ur": ("sbuf", [128, 128], CODES), "urs": ("sbuf", [128, 128], PLANE),
    "wq": ("sbuf", [128, 128], CODES), "ws": ("sbuf", [128, 128], PLANE),
    "kq": ("sbuf", [128, 576], CODES), "kp": ("sbuf", [128, 576], PLANE),
    "pq": ("sbuf", [128, 128], CODES), "ps": ("sbuf", [128, 128], PLANE),
    "fwl": ("dram", [128, 1], "int32"), "fwq": ("sbuf", [128, 32], CODES), "fws": ("sbuf", [128, 32], PLANE),
    "land": ("dram", [8, 128, 1], "int32"), "row": _i32(1024), "rowb": _i32(128),
    "lq": ("sbuf", [128, 128], CODES), "ls": ("sbuf", [128, 128], PLANE),
    "oq": ("sbuf", [128, 512], CODES), "op": ("sbuf", [128, 512], PLANE),
    "lst": _u16(8), "lo": _u16(2), "zo": _u16(8), "coff": _u16(4), "loff": _u16(32), "roff": _u16(16),
    "qall": _u16(2), "qown": _u16(2), "gl": _u16(4),
    "pf": _f32(1), "pw": _i32(8), "xa": _i32(2), "xb": _i32(2), "bt": _i32(8), "bs": _i32(4), "pm": _i32(1), "pmf": _f32(1),
    "pj": _f32(1), "qs": _f32(2), "q64": _f32(32), "jw": _f32(64), "kb": _f32(4), "tri": _b16(128), "ntri": _b16(128),
    "col": _f32(128), "colt": _f32(128),
    "c0": _b16(256), "c1": _b16(256), "c2": _b16(512), "c3": _b16(512), "zd": _b16(512), "zz": _b16(512), "zj": _b16(512),
    "part": _f32(2), "so": _b16(1056), "mt": _b16(32), "mg": _b16(64), "rr": _b16(64),
    "l1": _f32(32), "l2": _f32(64), "l3": _f32(64),
    "fl": _b16(128), "pinc": _b16(128), "zq": _f32(256), "junk": _b16(384), "junv": _b16(128),
    "evw": _f32(576), "e1": _f32(64), "e2": _f32(64), "yb": _f32(512),
    "pc": ("psum", [128, 2048], "float32"), "ra": ("psum", [128, 1024], "float32"), "rb": ("psum", [128, 1024], "float32"),
}
SEMAPHORES = ["sv", "ss", "st", "sg", "dsn", "dsd", "dx", "du", "dka", "dkb", "dw", "down", "drow", "dout",
              "aL", "aC", "aS", "fC", "fS", "loc"]


def bits(es):
    m = 0
    for e in es:
        m |= 1 << e
    return m


def u8(v):
    return v.bitcast(dt.uint8)


def u32(v):
    return v.bitcast(dt.uint32)


def split(es, n, turn=0):
    if n == 1:
        return [es]
    h = len(es) // 2
    if n == 2:
        return [es[:h], es[h:]]
    q = h // 2
    wide, rest = (es[:h], [es[h:h + q], es[h + q:]]) if turn % 2 == 0 else (es[h:], [es[:q], es[q:h]])
    return rest[:turn] + [wide] + rest[turn:]


def plan(s, T, topo):
    core = T.cores[s]
    n = len(T.cores)
    cross = [d for d in range(n) if d != s and not topo.may_write(core, T.cores[d])]
    home = [d for d in range(n) if d not in cross]
    same = [d for d in home if d != s]
    chip = [f for f in topo.cores_of(core) if f != core]
    ports = [f for f in chip if all(topo.may_write(f, T.cores[d]) for d in cross)]
    near = [f for f in ports if topo.die(f) == topo.die(core)]
    far = [f for f in ports if topo.die(f) != topo.die(core)]
    a, b = (near, far) if (s // 2) % 2 == 0 else (far, near)
    off = topo.engines(core, T.cores[same[0]])
    on = [e for e in topo.engines(core, near[0]) if e not in off]
    h = len(on) // 2
    hop = [(k, es, f, ds) for i, k in enumerate("CS") for es, f, ds in ((on[:h], a[i], cross[:2]), (on[h:], b[i], cross[2:]))]
    straight = [(k, es, d) for i, k in enumerate("CS") for es, d in zip(split(off, 3, i), same)]
    return {"core": core, "cross": cross, "home": home, "same": same, "order": cross + home, "on": on, "off": off,
            "list": list(zip([a[0], a[1], b[0], b[1]], cross)), "hop": hop, "straight": straight}


def last_leg(f, ds, T, topo):
    return split(topo.engines(f, T.cores[ds[0]]), len(ds))


def xfer(src_core, dst_cores, es, sem, src, dsts, topo):
    ids = []
    for d in dst_cores:
        rid, pid = topo.addr(d, src_core)
        ids.append(DstId(rid=rid, pnc=pid))
    return RemoteDMATransfer(dst_ids=ids, dma_engine_mask=bits(es), remote_sem=sem, srcs=[src], dsts=dsts)


def part(T, k, codes, plane, i, n):
    return u8(T[codes][:, 16 * i:16 * (i + n)]) if k == "C" else T[plane][:, 16 * i:16 * (i + n)]


def forward(g, core, s, T, topo):
    p = plan(s, T, topo)
    loc = 0
    for f, d in p["list"]:
        if f == core:
            es = topo.engines(core, T.cores[d])[:1]
            g.wait_ge(T.sem.aL, 1)
            g.remote_dma_fused([xfer(core, [T.cores[d]], es, T.sem.aL, T.fwl[:, :], [T.land[s]], topo)], local_sem=T.sem.loc)
            loc += len(es)
    for k, es, f, ds in p["hop"]:
        if f == core:
            g.wait_ge(T.sem["f" + k], len(es))
            ts = []
            for i, (d, me) in enumerate(zip(ds, last_leg(core, ds, T, topo))):
                ts.append(xfer(core, [T.cores[d]], me, T.sem["a" + k], part(T, k, "fwq", "fws", i, 1),
                               [part(T, k, "lq", "ls", s, 1)], topo))
                loc += len(me)
            g.remote_dma_fused(ts, local_sem=T.sem.loc)
    if loc:
        g.wait_ge(T.sem.loc, loc)


def rank_program(g, core, T, topo):
    r = T.rank_of(core)
    n = len(T.cores)
    if r is None:
        for s in range(n):
            if T.cores[s] in topo.cores_of(core):
                forward(g, core, s, T, topo)
        return
    P = plan(r, T, topo)
    V, S, E, Y = g.vector, g.scalar, g.tensor, g.sync
    sem = T.sem
    queue = {"v": V, "s": S, "t": E, "g": g, "y": Y}
    cnt = {"v": 0, "s": 0, "t": 0, "g": 0}
    seen = {}

    def w(name, *tags):
        for sn, val in tags:
            if seen.get((name, sn), 0) < val:
                queue[name].wait_ge(sem[sn], val)
                seen[(name, sn)] = val

    def do(name, call, tags):
        w(name, *tags)
        call().then_inc(sem["s" + name], 1)
        cnt[name] += 1
        return ("s" + name, cnt[name])

    def v(call, *tags):
        return do("v", call, tags)

    def sc(call, *tags):
        return do("s", call, tags)

    def mm(call, *tags):
        return do("t", call, tags)

    def gg(call, *tags):
        return do("g", call, tags)

    def ts(out, in0, s1, op0, s2=None, op1=None, tags=()):
        if op1 is None:
            return v(lambda: V.tensor_scalar(out, in0, s1, None, op0), *tags)
        return v(lambda: V.tensor_scalar(out, in0, s1, s2, op0, op1), *tags)

    def tt(out, in0, in1, op, *tags):
        return v(lambda: V.tensor_tensor(out, in0, in1, op), *tags)

    def cp(out, in_, *tags):
        return v(lambda: V.tensor_copy(out, in_), *tags)

    def act(out, in_, func, *tags, **kw):
        return sc(lambda: S.activation(out, in_, func, **kw), *tags)

    need = {"L": n - 1, "C": 0, "S": 0}
    for s in range(n):
        if s == r:
            continue
        p = plan(s, T, topo)
        for k, es, f, ds in p["hop"]:
            if r in ds:
                need[k] += len(last_leg(f, ds, T, topo)[ds.index(r)])
        for k, es, d in p["straight"]:
            if d == r:
                need[k] += len(es)

    Y.dma_start(T.snd[:, :], T.sn[:, :]).then_inc(sem.dsd, 16)
    S.dma_start(T.xt[:, :], T.x[:, :]).then_inc(sem.dx, 16)
    Y.dma_start(T.ut[:, 0:8], T.u[:, 0:8]).then_inc(sem.du, 16)
    for k in range(8):
        (Y if k < 4 else S).dma_start(T.snr[16 * k:16 * k + 16, :], T.sn[:, :]).then_inc(sem.dsn, 16)
    S.dma_start(T.kp[:, 64:576], T.ks[:, :]).then_inc(sem.dka, 16)
    Y.dma_start(u8(T.kq[:, 64:320]), T.kc[:, 0:1024]).then_inc(sem.dka, 16)
    Y.dma_start(u8(T.kq[:, 320:576]), T.kc[:, 1024:2048]).then_inc(sem.dkb, 16)
    Y.dma_start(T.land[r], T.sn[:, :]).then_inc(sem.down, 16)
    SN, DX, DU, DKA, DKB, DW = ("dsn", 128), ("dx", 16), ("du", 16), ("dka", 32), ("dkb", 16), ("dw", 16)

    a_pf = gg(lambda: g.iota(T.pf[:, :], [[1, 1]], 0, 1, allow_small_or_imprecise_dtypes=True))
    a_q = gg(lambda: g.iota(T.q64[:, :], [[16, 32]], 0, 0, allow_small_or_imprecise_dtypes=True))
    a_tri = gg(lambda: g.iota(T.tri[:, :], [[1, 128]], 0, -1, allow_small_or_imprecise_dtypes=True))
    a_u0 = v(lambda: V.memset(T.ut[:, 8:512], 0.0))
    a_zo = v(lambda: V.memset(T.zo[:, :], 0))
    a_c0 = v(lambda: V.memset(T.col[:, :], 0.0))
    a_pw = ts(T.pw[:, :], T.q64[:, 0:8], 16.0, A.add, T.pf[:, 0:1], A.mult, (a_pf, a_q))
    t = ts(T.pm[:, :], T.pw[:, 0:1], 4, A.logical_shift_right, 15, A.bitwise_and, (a_pw,))
    t1 = ts(T.xa[:, :], T.pw[:, 0:2], 0x440, A.bitwise_and)
    a_pm = ts(T.pmf[:, :], T.pm[:, :], 64.0, A.add, tags=(t,))
    a_xb = ts(T.xb[:, :], T.xa[:, :], 17, A.mult, tags=(t1,))
    pieces = [(T.bt[:, 0:1], T.xb[:, 0:1], 8, 4), (T.bt[:, 1:2], T.pw[:, 0:1], 7, 1), (T.bt[:, 2:3], T.pw[:, 3:4], 3, 48),
              (T.bt[:, 3:4], T.xb[:, 1:2], 7, 8), (T.bt[:, 4:5], T.pw[:, 1:2], 0, 32), (T.bt[:, 5:6], T.pw[:, 0:1], 7, 12),
              (T.bs[:, 3:4], T.pw[:, 1:2], 4, 2)]

    def piece():
        o, src, sh, mask = pieces.pop()
        return ts(o, src, sh, A.logical_shift_right, mask, A.bitwise_and, (a_xb,))

    t = act(T.pj[:, :], T.pf[:, :], F.Identity, a_pf, bias=0.75)
    a_cj = act(T.col[:, 0:128:32], T.q64[:, 0:4], F.Identity, t, a_q, a_c0, bias=T.pj[:, 0:1], scale=8.0)

    def pick(o, oc, i, ic, off, lc, vt, st):
        x = v(lambda: V.tensor_copy(u32(T[o[0]][:, oc[0]:oc[1]]), u32(T[i[0]][:, ic[0]:ic[1]]).indirect(T[off][:, lc[0]:lc[1]])), *vt)
        y = sc(lambda: S.activation(T[o[1]][:, oc[0]:oc[1]], T[i[1]][:, ic[0]:ic[1]].indirect(T[off][:, lc[0]:lc[1]]), F.Copy), *st)
        return x, y

    a_uq = v(lambda: V.quantize_mx(T.uq[:, :], T.us[:, :], T.ut[:, :]), DU, a_u0)
    cx, hm = P["cross"], P["home"]
    stx, sth = cx[1] - cx[0], hm[1] - hm[0]
    a_lx = cp(T.lst[:, 0:4], T.snr[:, cx[0]:cx[0] + 3 * stx + 1:stx], SN)
    a_ly = cp(T.lst[:, 4:8], T.snr[:, hm[0]:hm[0] + 3 * sth + 1:sth])
    a_lo = cp(T.lo[:, 0:1], T.snr[:, r:r + 1])
    ur = pick(("ur", "urs"), (0, 128), ("uq", "us"), (0, 128), "zo", (0, 8), (a_uq, a_zo), (a_uq, a_zo))
    a_xq = v(lambda: V.quantize_mx(T.xq[:, :], T.xs[:, :], T.xt[:, :]), DX)
    piece()
    piece()
    X, XW = ("xq", "xs"), (0, 128)
    px = pick(("pq", "ps"), (0, 64), X, XW, "lst", (0, 4), (a_xq, a_lx), (a_xq, a_lx))
    py = pick(("pq", "ps"), (64, 128), X, XW, "lst", (4, 8), (a_ly,), (a_ly,))
    po = pick(("lq", "ls"), (16 * r, 16 * r + 16), X, XW, "lo", (0, 1), (a_lo,), (a_lo,))

    loc = 0

    def send(tr, es):
        g.remote_dma_fused(tr, local_sem=sem.loc)
        return sum(len(e) for e in es)

    def hop(k):
        calls = [c for c in P["hop"] if c[0] == k]
        return send([xfer(core, [f], es, sem["f" + k], part(T, k, "pq", "ps", P["order"].index(ds[0]), 2),
                          [part(T, k, "fwq", "fws", 0, 2)], topo) for _, es, f, ds in calls], [c[1] for c in calls])

    def straight(k):
        calls = [c for c in P["straight"] if c[0] == k]
        return send([xfer(core, [T.cores[d]], es, sem["a" + k], part(T, k, "pq", "ps", P["order"].index(d), 1),
                          [part(T, k, "lq", "ls", r, 1)], topo) for _, es, d in calls], [c[1] for c in calls])

    w("g", ("dsd", 16))
    fs = [f for f, d in P["list"]]
    le = [P["on"][:1], P["off"][:1]]
    loc += send([xfer(core, fs, le[0], sem.aL, T.snd[:, :], [T.fwl[:, :] for f in fs], topo),
                 xfer(core, [T.cores[d] for d in P["same"]], le[1], sem.aL, T.snd[:, :], [T.land[r] for d in P["same"]], topo)], le)
    w("g", px[0])
    loc += hop("C")
    w("g", px[1])
    loc += hop("S")
    w("g", py[0])
    loc += straight("C")
    w("g", py[1])
    loc += straight("S")

    a_nt = ts(T.ntri[:, :], T.tri[:, :], 0.0, A.is_ge, 0.5, A.subtract, (a_tri,))
    a_m0 = v(lambda: V.memset(T.so[:, 1040:1056], 0.0))
    piece()
    piece()

    def scores(h, rows, *tags):
        lo = 64 + 256 * h
        for c in range(2):
            a = mm(lambda: E.matmul_mx(T.pc[:, 512 * (2 * h + c):512 * (2 * h + c) + 128], T.kq[:, lo + 128 * c:lo + 128 * c + 128],
                                       T.kp[:, lo + 128 * c:lo + 128 * c + 128], T.uq[:, :], T.us[:, :], True, True), *tags)
        b = [mm(lambda: E.matmul_mx(rows[:, 512 * k:512 * k + 256], T.ur[:, :], T.urs[:, :], T.kq[:, lo:lo + 256],
                                    T.kp[:, lo:lo + 256], True, True), *ur) for k in range(2)]
        return a, b[0], b[1]

    ca, ras, rav = scores(0, T.ra, DKA, a_uq)
    cb, rbs, rbv = scores(1, T.rb, DKB)

    def sj(c):
        return T.col[:, 32 * c + 1:32 * c + 2]

    sa = act(T.col[:, 1:64:32], T.pc[:, 0:1024:512], F.Copy, ca, a_cj)
    z = {}
    for c in (0, 1):
        z[c] = act(T.zd[:, 128 * c:128 * c + 128], T.ra[:, 128 * c:128 * c + 128], F.Sign, sa, ras, bias=sj(c), scale=-1.0)
    sb = act(T.col[:, 65:128:32], T.pc[:, 1024:2048:512], F.Copy, cb)
    S.dma_start(T.wt[:, :], T.w[:, :]).then_inc(sem.dw, 16)
    for c in (2, 3):
        z[c] = act(T.zd[:, 128 * c:128 * c + 128], T.rb[:, 128 * c - 256:128 * c - 128], F.Sign, sb, rbs, bias=sj(c), scale=-1.0)
    zz = [act(T.zz[:, 256 * c:256 * c + 256], T.rb[:, 0:256], F.Sign, bias=sj(c), scale=-1.0) for c in (0, 1)]
    pa = [act(T.zj[:, 256 * c:256 * c + 256], T.zz[:, 256 * c:256 * c + 256], F.Relu, zz[c], accum_out=T.part[:, c:c + 1])
          for c in (0, 1)]

    ts(T.c0[:, 128:256], T.ra[:, 640:768], sj(0), A.is_lt, tags=(sa, rav))
    ts(T.c1[:, 128:256], T.ra[:, 512:640], sj(1), A.is_le)
    tt(T.c0[:, 0:128], T.zd[:, 0:128], T.ntri[:, :], A.is_gt, z[0], a_nt)
    d01 = tt(T.c1[:, 0:128], T.zd[:, 128:256], T.ntri[:, :], A.is_gt, z[1])
    ts(T.c2[:, 0:256], T.ra[:, 512:768], sj(2), A.is_le, tags=(sb,))
    ts(T.c3[:, 0:256], T.ra[:, 512:768], sj(3), A.is_le)
    ts(T.c2[:, 384:512], T.rb[:, 640:768], sj(2), A.is_lt, tags=(rbv,))
    ts(T.c3[:, 256:384], T.rb[:, 512:640], sj(3), A.is_le)
    d2 = tt(T.c2[:, 256:384], T.zd[:, 256:384], T.ntri[:, :], A.is_gt, z[2])
    d3 = tt(T.c3[:, 384:512], T.zd[:, 384:512], T.ntri[:, :], A.is_gt, z[3])

    def total(c, k, first, *tags):
        b = T["c%d" % c]
        return v(lambda: V.tensor_tensor_scan(T.so[:, 1028 - 4 * k + c:1028:4], b[:, 0:k], b[:, k:2 * k], first,
                                              A.add, A.add), *tags)

    piece()
    total(2, 256, 0.0, d2)
    total(3, 256, 0.0, d3)
    total(0, 128, T.part[:, 0:1], pa[0], d01)
    a_so = total(1, 128, T.part[:, 1:2], pa[1])

    def mp(p0, p1, c0, c1):
        return T.so[p0:p1, 1024 + c0:1024 + c1]

    piece()
    a_bt = piece()
    t = cp(mp(0, 64, 4, 8), mp(64, 128, 0, 4), a_so)
    t1 = act(mp(64, 128, 4, 8), mp(0, 64, 0, 4), F.Copy, a_so)
    for k in range(2):
        a_gl = ts(T.gl[:, k:4:2], T.q64[:, 0:2], -64.0, A.add, T.pmf[:, 0:1], A.add, (a_pm,))
    cp(mp(0, 32, 8, 16), mp(32, 64, 0, 8), t)
    t = cp(mp(32, 64, 8, 16), mp(0, 32, 0, 8))
    a_j0 = act(T.jw[:, 0:64:2], T.q64[:, :], F.Identity, scale=0.0)
    act(mp(64, 96, 8, 16), mp(96, 128, 0, 8), F.Copy, t1)
    t1 = act(mp(96, 128, 8, 16), mp(64, 96, 0, 8), F.Copy)
    a_jw = act(T.jw[:, 1:64:2], T.q64[:, :], F.Identity, a_pm, bias=T.pmf[:, 0:1])
    a_w0 = act(T.evw[:, 0:64], T.tri[:, 0:64], F.Identity, a_tri, scale=0.0)
    a_kb = act(T.kb[:, :], T.jw[:, 1:8:2], F.Identity, a_jw, bias=-63.5)
    for a in range(4):
        a_w1 = act(T.evw[32 * a:32 * a + 1, 0:64], T.evw[32 * a:32 * a + 1, 0:64], F.Identity, a_w0, bias=-0.25)
    t2 = tt(T.bs[:, 0:3], T.bt[:, 0:3], T.bt[:, 3:6], A.add, a_bt)
    t = v(lambda: V.transpose(T.mt[:, :], mp(0, 128, 0, 32)), t, t1, a_m0)
    a_qs = tt(T.qs[:, :], T.bs[:, 0:4:2], T.bs[:, 1:4:2], A.add, t2)
    t = cp(T.mg[:, :], T.mt[:, :].indirect(T.gl[:, 0:4]), t, a_gl)
    a_qa = ts(T.qall[:, :], T.q64[:, 0:2], 0.125, A.mult, T.qs[:, 0:1], A.add, (a_qs,))
    a_v0 = v(lambda: V.memset(T.junv[:, 127:128], 0.0))
    a_rr = v(lambda: V.transpose(T.rr[:, :], T.mg[:, :]), t)
    a_wq = v(lambda: V.quantize_mx(T.wq[:, :], T.ws[:, :], T.wt[:, :]), DW)
    a_l1 = ts(T.l1[:, :], T.rr[:, :].indirect(T.qall[:, 0:2]), 64.0, A.min, tags=(a_rr, a_qa))
    ts(T.l2[:, 1:64:2], T.rr[:, :].indirect(T.qall[:, 0:2]), 64.0, A.min)

    w("y", ("aL", need["L"]), ("down", 16))
    Y.dma_start(T.row[0:1, :], T.land[:, :, :]).then_inc(sem.drow, 16)
    a_b = gg(lambda: g.partition_broadcast(T.rowb[:, :], T.row[0:1, r:1024:8], 128), ("drow", 16))
    t = ts(T.fl[:, :], T.rowb[:, :], 0, A.is_ge, tags=(a_b,))
    a_qo = ts(T.qown[:, 0:1], T.qs[:, 1:2], 1.0, A.add)
    a_pinc = v(lambda: V.tensor_tensor_scan(T.pinc[:, :], T.fl[:, :], T.fl[:, :], 0.0, A.add, A.max), t)
    a_ct = v(lambda: V.transpose(T.colt[:, :], T.col[:, :]), sb)
    m = T.pinc[:, 127:128]
    for q in range(3):
        a_z = act(T.junk[:, 128 * q:128 * q + 127], T.pinc[:, 0:127], F.Sign, a_pinc, a_kb, bias=T.kb[:, q:q + 1], scale=-1.0,
                  accum_out=T.zq[:, 64 * q + 63:64 * q + 64])
    t = ts(T.l2[:, 0:64:2], T.l1[:, :], m, A.is_ge, tags=(a_pinc,))
    t1 = ts(T.junv[:, 0:127], T.pinc[:, 0:127], T.kb[:, 3:4], A.is_le, 2.0, A.mult, (a_kb,))
    t = v(lambda: V.tensor_tensor_scan(T.l3[:, :], T.jw[:, :], T.l2[:, :], 0.0, A.mult, A.max), t, a_jw)
    t1 = v(lambda: V.tensor_tensor_scan(T.zq[:, 192:256], T.junv[:, 0:64], T.junv[:, 64:128], -127.0, A.add, A.add), t1)
    a_loff = cp(T.loff[:, :], T.l3[:, 1:64:2], t)
    a_roff = cp(T.roff[:, :], T.l3[:, :].indirect(T.qown[:, 0:1]))
    a_coff = ts(T.coff[:, :], T.zq[:, 63:256:64], 0.5, A.mult, 63.5, A.add, (a_z, t1))

    cc, cs = pick(("kq", "kp"), (0, 64), ("lq", "ls"), (0, 128), "coff", (0, 4),
                  (("aC", need["C"]), po[0], a_coff), (("aS", need["S"]), po[1], a_coff))
    fin = []
    for h in range(2):
        fin.append(pick(("oq", "op"), (256 * h, 256 * h + 256), ("kq", "kp"), (0, 576), "loff", (16 * h, 16 * h + 16),
                        (cc, a_loff), (cs, a_loff)))
    yc = []
    for h in range(2):
        lo, hi = 256 * h, 256 * h + 256
        ym = mm(lambda: E.matmul_mx(T.pc[:, 512 * h:512 * h + 256], T.wq[:, :], T.ws[:, :], T.oq[:, lo:hi], T.op[:, lo:hi],
                                    True, True), a_wq, *fin[h])
        yc.append(act(T.yb[:, lo:hi], T.pc[:, 512 * h:512 * h + 256], F.Copy, ym))
    t = cp(T.evw[:, :].indirect(T.roff[:, 0:8]), T.colt[:, :], a_roff, a_ct, a_w1)
    t = tt(T.e1[0:64, :], T.evw[0:64, 0:64], T.evw[64:128, 0:64], A.add, t)
    a_ev = tt(T.e2[0:32, :], T.e1[0:32, :], T.e1[32:64, :], A.add, t)

    outs = [0]

    def store(nm, tag, o, i):
        w(nm, tag)
        queue[nm].dma_start(o, i).then_inc(sem.dout, 16)
        outs[0] += 16

    for h in range(2):
        store("y", fin[h][0], T.oc[:, 1024 * h:1024 * h + 1024], u8(T.oq[:, 256 * h:256 * h + 256]))
    store("y", yc[0], T.y[:, 0:256], T.yb[:, 0:256])
    store("y", yc[1], T.y[:, 256:512], T.yb[:, 256:512])
    for k in range(4):
        store("s", fin[1][1], T.osc[4 * k:4 * k + 4, :], T.op[32 * k:32 * k + 4, :])
    store("y", a_ev, T.ev[:, :], T.e2[0:2, :])

    w("g", ("sv", cnt["v"]), ("ss", cnt["s"]), ("st", cnt["t"]), ("sg", cnt["g"]), ("dout", outs[0]), ("loc", loc))
